import numpy as np
import ml_dtypes


def mxq(x, axis, fmt="e4m3"):
    dtype, down = {"e4m3": (ml_dtypes.float8_e4m3fn, 7), "e5m2": (ml_dtypes.float8_e5m2, 14)}[fmt]
    v = np.moveaxis(np.asarray(x, np.float32).astype(ml_dtypes.bfloat16).astype(np.float64), axis, -1)
    blocks = v.reshape(v.shape[:-1] + (-1, 32))
    amax = np.abs(blocks).max(-1, keepdims=True)
    byte = np.maximum(np.where(amax > 0, np.frexp(amax)[1] - 1 + 127, 0) - down, 1)
    scale = np.exp2(byte - 127.0)
    codes = (blocks / scale).astype(np.float32).astype(dtype).astype(np.float64)
    return np.moveaxis((codes * scale).reshape(v.shape), -1, axis)


WIDE = False


def mx_kscale(k):
    if not WIDE:
        return np.ones(k)
    levels = np.array([18, -18])
    if k % 512:
        return np.exp2(np.random.permutation(np.resize(levels, k // 32))).repeat(32)
    a = np.empty((k // 512, 16))
    for p in range(k // 512):
        a[p, :8] = np.random.permutation(np.resize(levels, 8))
        for g in range(8):
            far = levels[np.abs(levels - a[p, g]) >= 10]
            a[p, g + 8] = far[np.random.randint(len(far))]
    return np.exp2(a.ravel()).repeat(32)


def f64(x):
    return np.asarray(x).astype(np.float64)


def striped(idx):
    return np.tile(np.asarray(idx).reshape(-1, 16).T, (8, 1)).astype(np.uint16)


def unstriped(offs):
    return offs[:16].T.reshape(-1).astype(np.int64)


B, N, T, D, R = 1, 512, 2048, 512, 1024


def setup_inputs():
    n = np.random.standard_normal
    idx = np.random.permutation(T)[:B * N]
    s = mx_kscale(D)[:, None]
    u = np.ones(T)
    u[idx] = mx_kscale(B * N)
    r = np.random.uniform(0.5, 2.0, T) * u
    x = n((B, D, R))
    return {
        "xT": (x * s).astype(np.float32),
        "wT": (n((D, T)) * (1.00 / np.sqrt(D)) / s / r).astype(np.float32),
        "y": n((B, R, N)).astype(np.float32),
        "wt": (np.random.uniform(0.5, 1.5, (B, R, 1)) * 1.0 / np.sqrt(R)).astype(np.float32),
        "ts": np.tile(r, (128, 1)).astype(np.float32),
        "offs": striped(idx),
    }


def reference(xT, wT, y, wt, ts, offs):
    idx = unstriped(offs)
    pick = lambda x: x[:, idx].reshape(x.shape[0], B, N).transpose(1, 0, 2)
    w = pick(f64(wT))
    a = mxq(f64(xT), 1, "e4m3").transpose(0, 2, 1) @ mxq(w, 1, "e4m3")
    ts_ = pick(f64(ts))[:, :1, :]
    a = a * ts_
    g = f64(wt) * np.tanh(a - f64(y))
    g = g * ts_
    gx = mxq(g, 2, "e5m2") @ mxq(w, 2, "e4m3").transpose(0, 2, 1)
    return gx

@@ -1,0 +1,218 @@
+from contextlib import ExitStack
+
+import concourse.mybir as mybir
+from concourse.masks import make_identity
+
+N, T, D, R = 512, 2048, 512, 1024
+FLOPS = 2 * 2 * R * N * D
+BYTES = 4 * (D * R + D * T + R * N + R + T + R * D) + 2 * 128 * (N // 16)
+
+F32 = mybir.dt.float32
+BF16 = mybir.dt.bfloat16
+U32 = mybir.dt.uint32
+U16 = mybir.dt.uint16
+U8 = mybir.dt.uint8
+E4M3 = mybir.dt.float8_e4m3fn_x4
+E5M2 = mybir.dt.float8_e5m2_x4
+ACT = mybir.ActivationFunctionType
+MULT = mybir.AluOpType.mult
+
+P = 128
+PACK = 4
+PAIR = 2
+PAIRS = R // (P * PAIR)
+CHUNKS = PAIRS * PAIR
+
+
+def tile_attend_glch_x_ts_kernel(tc, xT, wT, y, wt, ts, offs, out):
+    nc = tc.nc
+    with ExitStack() as ctx:
+        keep = ctx.enter_context(tc.tile_pool(name="keep", bufs=1))
+        ring = ctx.enter_context(tc.tile_pool(name="ring", bufs=4))
+        psum = ctx.enter_context(tc.psum_pool(name="psum", bufs=2))
+
+        offsets = keep.tile([P, N // 16], U16, name="offsets")
+        nc.sync.dma_start(offsets[:], offs)
+        wt_sb = keep.tile([P, PAIRS, PAIR], F32, name="wt_sb")
+        nc.sync.dma_start(wt_sb[:], wt[0].rearrange("(c p j) o -> p c (j o)", p=P, j=PAIR))
+        w_rows = wT.rearrange("(p t) c -> t p c", t=PACK)
+        w_plane = [ring.tile([P, T], F32, name="w_plane%d" % t, tag="stage") for t in range(PACK)]
+        for t in range(PACK):
+            nc.sync.dma_start(w_plane[t][:], w_rows[t])
+        x_rows = xT[0].rearrange("(p t) r -> p t r", t=PACK)
+        y_rows = y[0].rearrange("(c p j) i -> c p j i", p=P, j=PAIR)
+        out_rows = out[0].rearrange("(c p j) d -> c p j d", p=P, j=PAIR)
+        x_raw = {}
+        y_sb = {}
+
+        def load_rows(c):
+            x_raw[c] = ring.tile([P, PACK, P * PAIR], F32, name="x_raw", tag="stage")
+            nc.sync.dma_start(x_raw[c][:], x_rows[:, :, c * P * PAIR : (c + 1) * P * PAIR])
+            y_sb[c] = ring.tile([P, PAIR, N], F32, name="y_sb", tag="stage")
+            nc.sync.dma_start(y_sb[c][:], y_rows[c])
+
+        ts_row = keep.tile([1, T], F32, name="ts_row")
+        nc.scalar.dma_start(ts_row[:], ts[0:1, :])
+        ts_window = keep.tile([P, T], F32, name="ts_window", tag="listed", align_bytes=64)
+        nc.vector.memset(ts_window[:], 0.0)
+        nc.vector.tensor_copy(ts_window[0:1, :], ts_row[:])
+
+        ident = keep.tile([P, P], F32, name="ident")
+        make_identity(nc, ident[:])
+        warm = keep.tile([P, 1], F32, name="warm")
+        nc.scalar.activation(warm[:], ident[:, 0:1], ACT.Tanh)
+        ident_bf = keep.tile([P, P], BF16, name="ident_bf")
+        make_identity(nc, ident_bf[:])
+
+        ts_listed = keep.tile([P, N], F32, name="ts_listed")
+        nc.vector.tensor_copy(ts_listed[:], ts_window[:].indirect(offsets[:]))
+        ts_turned = psum.tile([P, PACK, P], F32, name="ts_turned", tag="a")
+        for t in range(PACK):
+            nc.tensor.transpose(ts_turned[:, t, :], ts_listed[:, t::PACK], ident[:])
+        ts_part = keep.tile([P, PACK], F32, name="ts_part")
+        nc.scalar.copy(ts_part[:], ts_turned[:, :, 0])
+        ts_spread = psum.tile([P, PACK, P], F32, name="ts_spread", tag="a")
+        for t in range(PACK):
+            nc.tensor.transpose(ts_spread[:, t, :], ts_part[:, t : t + 1].to_broadcast([P, P]), ident[:])
+        neg_ts = keep.tile([P, PACK, P], F32, name="neg_ts")
+        nc.scalar.activation(neg_ts[:], ts_spread[:], ACT.Copy, scale=-1.0)
+
+        factor = keep.tile([P, CHUNKS, PACK, P], F32, name="factor")
+        wt_flat = wt_sb[:].rearrange("p c j -> p (c j)")
+        for half in range(2):
+            wt_spread = psum.tile([P, 4, P], F32, name="wt_spread", tag="z", bufs=4)
+            for k in range(4):
+                col = 4 * half + k
+                nc.tensor.transpose(wt_spread[:, k, :], wt_flat[:, col : col + 1].to_broadcast([P, P]), ident[:])
+            for t in range(PACK):
+                nc.scalar.activation(factor[:, 4 * half : 4 * half + 4, t, :], wt_spread[:], ACT.Copy,
+                                     scale=ts_part[:, t : t + 1])
+
+        w_listed = keep.tile([P, N, PACK], BF16, name="w_listed", tag="listed", align_bytes=64)
+        w_turned = keep.tile([P, PACK, P, PACK], BF16, name="w_turned", align_bytes=64)
+        wd_codes = keep.tile([P, N], U32, name="wd_codes", align_bytes=64)
+        wd_scales = keep.tile([P, N], U8, name="wd_scales", align_bytes=64)
+        wi_codes = keep.tile([P, D], U32, name="wi_codes", align_bytes=64)
+        wi_scales = keep.tile([P, D], U8, name="wi_scales", align_bytes=64)
+
+        def turn_plane(t):
+            bank = psum.tile([P, PACK, P], BF16, name="w_bank", tag="a" if t == 2 else "o")
+            for s in range(PACK):
+                nc.tensor.transpose(bank[:, s, :], w_listed[:, s::PACK, t], ident_bf[:])
+            nc.scalar.copy(w_turned[:, t], bank[:].rearrange("q s p -> q p s"))
+
+        def quantize_plane(t):
+            nc.vector.quantize_mx(out=wi_codes[:, t * P : (t + 1) * P].bitcast(E4M3),
+                                  scales=wi_scales[:, t * P : (t + 1) * P],
+                                  in_=w_turned[:, t].rearrange("q p s -> q (p s)"))
+
+        for t in range(PACK):
+            nc.vector.tensor_copy(w_listed[:, :, t], w_plane[t][:].indirect(offsets[:]))
+            if t < PACK - 1:
+                turn_plane(t)
+            if t > 0:
+                quantize_plane(t - 1)
+        nc.vector.quantize_mx(out=wd_codes[:].bitcast(E4M3), scales=wd_scales[:],
+                              in_=w_listed[:].rearrange("p i t -> p (i t)"))
+
+        x_codes = keep.tile([P, R], U32, name="x_codes", align_bytes=64)
+        x_scales = keep.tile([P, R], U8, name="x_scales", align_bytes=64)
+        x_grouped = {}
+        sums = {}
+        targets = {}
+        tanhs = {}
+        h_ops = {}
+
+        def interleave_x(c):
+            x_grouped[c] = ring.tile([P, PAIR, P, PACK], BF16, name="x_grouped", align_bytes=64)
+            nc.scalar.copy(x_grouped[c][:].rearrange("p j n t -> p n t j"),
+                           x_raw[c][:].rearrange("p t (n j) -> p n t j", j=PAIR))
+
+        def quantize_x(c):
+            cols = slice(c * PAIR * P, (c + 1) * PAIR * P)
+            nc.vector.quantize_mx(out=x_codes[:, cols].bitcast(E4M3), scales=x_scales[:, cols],
+                                  in_=x_grouped[c][:].rearrange("p j n t -> p (j n t)"))
+
+        def scores(c):
+            for j in range(PAIR):
+                k = c * PAIR + j
+                cols = slice(k * P, (k + 1) * P)
+                sums[k] = psum.tile([P, N], F32, name="a", tag="a")
+                nc.tensor.matmul_mx(out=sums[k][:], lhsT=x_codes[:, cols].bitcast(E4M3), lhsT_scale=x_scales[:, cols],
+                                    rhs=wd_codes[:].bitcast(E4M3), rhs_scale=wd_scales[:], start=True, stop=True)
+
+        def turn_targets(c):
+            for j in range(PAIR):
+                k = c * PAIR + j
+                targets[k] = psum.tile([P, PACK, P], F32, name="z", tag="z", bufs=4)
+                for t in range(PACK):
+                    nc.tensor.matmul(targets[k][:, t, :], y_sb[c][:, j, t::PACK], ident[:], start=(t == 0), stop=False,
+                                     is_transpose=True)
+
+        def residuals(c):
+            scaled = []
+            for j in range(PAIR):
+                k = c * PAIR + j
+                neg_a = ring.tile([P, PACK, P], F32, name="neg_a")
+                nc.vector.tensor_tensor(neg_a[:], sums[k][:].rearrange("r (p t) -> r t p", t=PACK), neg_ts[:], MULT)
+                scaled.append(neg_a)
+            for j in range(PAIR):
+                k = c * PAIR + j
+                for t in range(PACK):
+                    nc.tensor.matmul(targets[k][:, t, :], scaled[j][:, t, :], ident[:], start=False,
+                                     stop=(t == PACK - 1), is_transpose=True)
+                tanhs[k] = ring.tile([P, PACK, P], F32, name="tanh")
+                nc.scalar.activation(tanhs[k][:], targets[k][:], ACT.Tanh, scale=-1.0)
+
+        def weigh(c):
+            grouped = []
+            for j in range(PAIR):
+                k = c * PAIR + j
+                h = ring.tile([P, P, PACK], BF16, name="h", align_bytes=64)
+                nc.vector.tensor_tensor(h[:].rearrange("p (m i) t -> p m t i", i=4),
+                                        tanhs[k][:].rearrange("p t (m i) -> p m t i", i=4),
+                                        factor[:, k].rearrange("p t (m i) -> p m t i", i=4), MULT)
+                grouped.append(h)
+            for j in range(PAIR):
+                k = c * PAIR + j
+                h_codes = ring.tile([P, P], U32, name="h_codes", align_bytes=64)
+                h_scales = ring.tile([P, P], U8, name="h_scales", align_bytes=64)
+                nc.vector.quantize_mx(out=h_codes[:].bitcast(E5M2), scales=h_scales[:],
+                                      in_=grouped[j][:].rearrange("p n t -> p (n t)"))
+                h_ops[k] = (h_codes, h_scales)
+
+        def gradient(c):
+            result = ring.tile([P, PAIR, D], F32, name="result")
+            for j in range(PAIR):
+                h_codes, h_scales = h_ops[c * PAIR + j]
+                grad = psum.tile([P, D], F32, name="grad", tag="o")
+                nc.tensor.matmul_mx(out=grad[:], lhsT=h_codes[:].bitcast(E5M2), lhsT_scale=h_scales[:],
+                                    rhs=wi_codes[:].bitcast(E4M3), rhs_scale=wi_scales[:], start=True, stop=True)
+                natural = result[:, j, :].rearrange("r (p t) -> r p t", t=PACK)
+                planes = grad[:].rearrange("r (t p) -> r p t", t=PACK)
+                if c == PAIRS - 1 and j == PAIR - 1:
+                    nc.vector.tensor_copy(natural, planes)
+                else:
+                    nc.scalar.copy(natural, planes)
+                if c == PAIRS - 1:
+                    nc.sync.dma_start(out_rows[c][:, j, :], result[:, j, :])
+            if c < PAIRS - 1:
+                nc.sync.dma_start(out_rows[c], result[:])
+
+        def prepare(c):
+            load_rows(c)
+            interleave_x(c)
+            quantize_x(c)
+            scores(c)
+            turn_targets(c)
+
+        prepare(0)
+        turn_plane(PACK - 1)
+        residuals(0)
+        quantize_plane(PACK - 1)
+        for c in range(PAIRS):
+            if c + 1 < PAIRS:
+                prepare(c + 1)
+                residuals(c + 1)
+            weigh(c)
+            gradient(c)

@@ -20,8 +20,9 @@ MULT = mybir.AluOpType.mult
 P = 128
 PACK = 4
 PAIR = 2
-PAIRS = R // (P * PAIR)
-CHUNKS = PAIRS * PAIR
+CHUNKS = R // P
+LOADS = "x0 y0 x1 x2 y1 x3 y2 y3".split()
+ORDER = "j0 w0 j1 w1 m0 p1 p2 j2 y0 t3 B0 w2 U0 p3 m1 j3 y1 B1 w3 U1 m2 j4 y2 B2 w4 U2 m3 D0 j5 y3 B3 w5 q0 U3 m4 D1 j6 y4 B4 w6 q1 U4 m5 D2 j7 G0 y5 B5 w7 q2 U5 m6 D3 G1 y6 B6 q3 U6 m7 D4 G2 y7 B7 q4 U7 D5 G3 q5 D6 G4 q6 D7 G5 q7 G6 G7".split()
 
 
 def tile_attend_glch_x_ts_kernel(tc, xT, wT, y, wt, ts, offs, out):
@@ -29,27 +30,19 @@ def tile_attend_glch_x_ts_kernel(tc, xT, wT, y, wt, ts, offs, out):
     with ExitStack() as ctx:
         keep = ctx.enter_context(tc.tile_pool(name="keep", bufs=1))
         ring = ctx.enter_context(tc.tile_pool(name="ring", bufs=4))
-        psum = ctx.enter_context(tc.psum_pool(name="psum", bufs=2))
+        psum = ctx.enter_context(tc.psum_pool(name="psum", bufs=1))
 
         offsets = keep.tile([P, N // 16], U16, name="offsets")
         nc.sync.dma_start(offsets[:], offs)
-        wt_sb = keep.tile([P, PAIRS, PAIR], F32, name="wt_sb")
-        nc.sync.dma_start(wt_sb[:], wt[0].rearrange("(c p j) o -> p c (j o)", p=P, j=PAIR))
+        wt_sb = keep.tile([P, R // P], F32, name="wt_sb")
+        nc.sync.dma_start(wt_sb[:], wt[0].rearrange("(p k) o -> p (k o)", p=P))
         w_rows = wT.rearrange("(p t) c -> t p c", t=PACK)
         w_plane = [ring.tile([P, T], F32, name="w_plane%d" % t, tag="stage") for t in range(PACK)]
         for t in range(PACK):
             nc.sync.dma_start(w_plane[t][:], w_rows[t])
         x_rows = xT[0].rearrange("(p t) r -> p t r", t=PACK)
-        y_rows = y[0].rearrange("(c p j) i -> c p j i", p=P, j=PAIR)
-        out_rows = out[0].rearrange("(c p j) d -> c p j d", p=P, j=PAIR)
-        x_raw = {}
-        y_sb = {}
-
-        def load_rows(c):
-            x_raw[c] = ring.tile([P, PACK, P * PAIR], F32, name="x_raw", tag="stage")
-            nc.sync.dma_start(x_raw[c][:], x_rows[:, :, c * P * PAIR : (c + 1) * P * PAIR])
-            y_sb[c] = ring.tile([P, PAIR, N], F32, name="y_sb", tag="stage")
-            nc.sync.dma_start(y_sb[c][:], y_rows[c])
+        y_rows = y[0].rearrange("(c j p) i -> c p j i", p=P, j=PAIR)
+        out_rows = out[0].rearrange("(k p) d -> k p d", p=P)
 
         ts_row = keep.tile([1, T], F32, name="ts_row")
         nc.scalar.dma_start(ts_row[:], ts[0:1, :])
@@ -66,27 +59,26 @@ def tile_attend_glch_x_ts_kernel(tc, xT, wT, y, wt, ts, offs, out):
 
         ts_listed = keep.tile([P, N], F32, name="ts_listed")
         nc.vector.tensor_copy(ts_listed[:], ts_window[:].indirect(offsets[:]))
-        ts_turned = psum.tile([P, PACK, P], F32, name="ts_turned", tag="a")
+        ts_turned = psum.tile([P, PACK, P], F32, name="ts_turned", tag="a", bufs=3)
         for t in range(PACK):
             nc.tensor.transpose(ts_turned[:, t, :], ts_listed[:, t::PACK], ident[:])
         ts_part = keep.tile([P, PACK], F32, name="ts_part")
         nc.scalar.copy(ts_part[:], ts_turned[:, :, 0])
-        ts_spread = psum.tile([P, PACK, P], F32, name="ts_spread", tag="a")
+        ts_spread = psum.tile([P, PACK, P], F32, name="ts_spread", tag="a", bufs=3)
         for t in range(PACK):
             nc.tensor.transpose(ts_spread[:, t, :], ts_part[:, t : t + 1].to_broadcast([P, P]), ident[:])
         neg_ts = keep.tile([P, PACK, P], F32, name="neg_ts")
         nc.scalar.activation(neg_ts[:], ts_spread[:], ACT.Copy, scale=-1.0)
 
-        factor = keep.tile([P, CHUNKS, PACK, P], F32, name="factor")
-        wt_flat = wt_sb[:].rearrange("p c j -> p (c j)")
+        factor = keep.tile([P, PACK, R], F32, name="factor")
         for half in range(2):
-            wt_spread = psum.tile([P, 4, P], F32, name="wt_spread", tag="z", bufs=4)
+            wt_spread = psum.tile([P, 4, P], F32, name="wt_spread", tag="z", bufs=2)
             for k in range(4):
                 col = 4 * half + k
-                nc.tensor.transpose(wt_spread[:, k, :], wt_flat[:, col : col + 1].to_broadcast([P, P]), ident[:])
+                nc.tensor.transpose(wt_spread[:, k, :], wt_sb[:, col : col + 1].to_broadcast([P, P]), ident[:])
             for t in range(PACK):
-                nc.scalar.activation(factor[:, 4 * half : 4 * half + 4, t, :], wt_spread[:], ACT.Copy,
-                                     scale=ts_part[:, t : t + 1])
+                nc.scalar.activation(factor[:, t, :].rearrange("p (n k) -> p n k", k=8)[:, :, 4 * half : 4 * half + 4],
+                                     wt_spread[:].rearrange("p k n -> p n k"), ACT.Copy, scale=ts_part[:, t : t + 1])
 
         w_listed = keep.tile([P, N, PACK], BF16, name="w_listed", tag="listed", align_bytes=64)
         w_turned = keep.tile([P, PACK, P, PACK], BF16, name="w_turned", align_bytes=64)
@@ -95,124 +87,123 @@ def tile_attend_glch_x_ts_kernel(tc, xT, wT, y, wt, ts, offs, out):
         wi_codes = keep.tile([P, D], U32, name="wi_codes", align_bytes=64)
         wi_scales = keep.tile([P, D], U8, name="wi_scales", align_bytes=64)
 
+        def gather_plane(t):
+            nc.vector.tensor_copy(w_listed[:, :, t], w_plane[t][:].indirect(offsets[:]))
+
         def turn_plane(t):
-            bank = psum.tile([P, PACK, P], BF16, name="w_bank", tag="a" if t == 2 else "o")
+            if t == 2:
+                bank = psum.tile([P, PACK, P], BF16, name="w_bank", tag="a", bufs=3)
+            else:
+                bank = psum.tile([P, PACK, P], BF16, name="w_bank", tag="o", bufs=3)
             for s in range(PACK):
                 nc.tensor.transpose(bank[:, s, :], w_listed[:, s::PACK, t], ident_bf[:])
-            nc.scalar.copy(w_turned[:, t], bank[:].rearrange("q s p -> q p s"))
+            if t in [0]:
+                nc.vector.tensor_copy(w_turned[:, t], bank[:].rearrange("q s p -> q p s"))
+            else:
+                nc.scalar.copy(w_turned[:, t], bank[:].rearrange("q s p -> q p s"))
 
         def quantize_plane(t):
             nc.vector.quantize_mx(out=wi_codes[:, t * P : (t + 1) * P].bitcast(E4M3),
                                   scales=wi_scales[:, t * P : (t + 1) * P],
                                   in_=w_turned[:, t].rearrange("q p s -> q (p s)"))
 
-        for t in range(PACK):
-            nc.vector.tensor_copy(w_listed[:, :, t], w_plane[t][:].indirect(offsets[:]))
-            if t < PACK - 1:
-                turn_plane(t)
-            if t > 0:
-                quantize_plane(t - 1)
+        gather_plane(0)
+        gather_plane(1)
+        turn_plane(0)
+        gather_plane(2)
+        turn_plane(1)
+        gather_plane(3)
+        turn_plane(2)
+        quantize_plane(0)
         nc.vector.quantize_mx(out=wd_codes[:].bitcast(E4M3), scales=wd_scales[:],
                               in_=w_listed[:].rearrange("p i t -> p (i t)"))
+
+        x_raw = {}
+        y_sb = {}
+        for item in LOADS:
+            c = int(item[1])
+            if item[0] == "x":
+                x_raw[c] = ring.tile([P, PACK, P * PAIR], F32, name="x_raw", tag="stage")
+                nc.sync.dma_start(x_raw[c][:], x_rows[:, :, c * P * PAIR : (c + 1) * P * PAIR])
+            else:
+                y_sb[c] = ring.tile([P, PAIR, N], F32, name="y_sb", tag="stage")
+                nc.sync.dma_start(y_sb[c][:], y_rows[c])
 
         x_codes = keep.tile([P, R], U32, name="x_codes", align_bytes=64)
         x_scales = keep.tile([P, R], U8, name="x_scales", align_bytes=64)
         x_grouped = {}
         sums = {}
         targets = {}
+        neg_a = {}
         tanhs = {}
+        h = {}
         h_ops = {}
 
-        def interleave_x(c):
-            x_grouped[c] = ring.tile([P, PAIR, P, PACK], BF16, name="x_grouped", align_bytes=64)
-            nc.scalar.copy(x_grouped[c][:].rearrange("p j n t -> p n t j"),
-                           x_raw[c][:].rearrange("p t (n j) -> p n t j", j=PAIR))
+        def interleave_x(k):
+            x_grouped[k] = ring.tile([P, P, PACK], BF16, name="x_grouped", align_bytes=64, bufs=6)
+            dst = x_grouped[k][:].rearrange("p (m i) t -> p m t i", i=4)
+            src = x_raw[k // PAIR][:, :, (k % PAIR) * P : (k % PAIR + 1) * P].rearrange("p t (m i) -> p m t i", i=4)
+            if k in []:
+                nc.vector.tensor_copy(dst, src)
+            else:
+                nc.scalar.copy(dst, src)
 
-        def quantize_x(c):
-            cols = slice(c * PAIR * P, (c + 1) * PAIR * P)
+        def quantize_x(k):
+            cols = slice(k * P, (k + 1) * P)
             nc.vector.quantize_mx(out=x_codes[:, cols].bitcast(E4M3), scales=x_scales[:, cols],
-                                  in_=x_grouped[c][:].rearrange("p j n t -> p (j n t)"))
+                                  in_=x_grouped[k][:].rearrange("p n t -> p (n t)"))
 
-        def scores(c):
-            for j in range(PAIR):
-                k = c * PAIR + j
-                cols = slice(k * P, (k + 1) * P)
-                sums[k] = psum.tile([P, N], F32, name="a", tag="a")
-                nc.tensor.matmul_mx(out=sums[k][:], lhsT=x_codes[:, cols].bitcast(E4M3), lhsT_scale=x_scales[:, cols],
-                                    rhs=wd_codes[:].bitcast(E4M3), rhs_scale=wd_scales[:], start=True, stop=True)
+        def scores(k):
+            cols = slice(k * P, (k + 1) * P)
+            sums[k] = psum.tile([P, N], F32, name="a", tag="a", bufs=3)
+            nc.tensor.matmul_mx(out=sums[k][:], lhsT=x_codes[:, cols].bitcast(E4M3), lhsT_scale=x_scales[:, cols],
+                                rhs=wd_codes[:].bitcast(E4M3), rhs_scale=wd_scales[:], start=True, stop=True)
 
-        def turn_targets(c):
-            for j in range(PAIR):
-                k = c * PAIR + j
-                targets[k] = psum.tile([P, PACK, P], F32, name="z", tag="z", bufs=4)
-                for t in range(PACK):
-                    nc.tensor.matmul(targets[k][:, t, :], y_sb[c][:, j, t::PACK], ident[:], start=(t == 0), stop=False,
-                                     is_transpose=True)
+        def turn_targets(k):
+            targets[k] = psum.tile([P, PACK, P], F32, name="z", tag="z", bufs=2)
+            for t in range(PACK):
+                nc.tensor.matmul(targets[k][:, t, :], y_sb[k // PAIR][:, k % PAIR, t::PACK], ident[:],
+                                 start=(t == 0), stop=False, is_transpose=True)
 
-        def residuals(c):
-            scaled = []
-            for j in range(PAIR):
-                k = c * PAIR + j
-                neg_a = ring.tile([P, PACK, P], F32, name="neg_a")
-                nc.vector.tensor_tensor(neg_a[:], sums[k][:].rearrange("r (p t) -> r t p", t=PACK), neg_ts[:], MULT)
-                scaled.append(neg_a)
-            for j in range(PAIR):
-                k = c * PAIR + j
-                for t in range(PACK):
-                    nc.tensor.matmul(targets[k][:, t, :], scaled[j][:, t, :], ident[:], start=False,
-                                     stop=(t == PACK - 1), is_transpose=True)
-                tanhs[k] = ring.tile([P, PACK, P], F32, name="tanh")
-                nc.scalar.activation(tanhs[k][:], targets[k][:], ACT.Tanh, scale=-1.0)
+        def scale_scores(k):
+            neg_a[k] = ring.tile([P, PACK, P], F32, name="neg_a")
+            nc.vector.tensor_tensor(neg_a[k][:], sums[k][:].rearrange("r (p t) -> r t p", t=PACK), neg_ts[:], MULT)
 
-        def weigh(c):
-            grouped = []
-            for j in range(PAIR):
-                k = c * PAIR + j
-                h = ring.tile([P, P, PACK], BF16, name="h", align_bytes=64)
-                nc.vector.tensor_tensor(h[:].rearrange("p (m i) t -> p m t i", i=4),
-                                        tanhs[k][:].rearrange("p t (m i) -> p m t i", i=4),
-                                        factor[:, k].rearrange("p t (m i) -> p m t i", i=4), MULT)
-                grouped.append(h)
-            for j in range(PAIR):
-                k = c * PAIR + j
-                h_codes = ring.tile([P, P], U32, name="h_codes", align_bytes=64)
-                h_scales = ring.tile([P, P], U8, name="h_scales", align_bytes=64)
-                nc.vector.quantize_mx(out=h_codes[:].bitcast(E5M2), scales=h_scales[:],
-                                      in_=grouped[j][:].rearrange("p n t -> p (n t)"))
-                h_ops[k] = (h_codes, h_scales)
+        def residual(k):
+            for t in range(PACK):
+                nc.tensor.matmul(targets[k][:, t, :], neg_a[k][:, t, :], ident[:], start=False,
+                                 stop=(t == PACK - 1), is_transpose=True)
+            tanhs[k] = ring.tile([P, PACK, P], F32, name="tanh")
+            nc.scalar.activation(tanhs[k][:], targets[k][:], ACT.Tanh, scale=-1.0)
 
-        def gradient(c):
-            result = ring.tile([P, PAIR, D], F32, name="result")
-            for j in range(PAIR):
-                h_codes, h_scales = h_ops[c * PAIR + j]
-                grad = psum.tile([P, D], F32, name="grad", tag="o")
-                nc.tensor.matmul_mx(out=grad[:], lhsT=h_codes[:].bitcast(E5M2), lhsT_scale=h_scales[:],
-                                    rhs=wi_codes[:].bitcast(E4M3), rhs_scale=wi_scales[:], start=True, stop=True)
-                natural = result[:, j, :].rearrange("r (p t) -> r p t", t=PACK)
-                planes = grad[:].rearrange("r (t p) -> r p t", t=PACK)
-                if c == PAIRS - 1 and j == PAIR - 1:
-                    nc.vector.tensor_copy(natural, planes)
-                else:
-                    nc.scalar.copy(natural, planes)
-                if c == PAIRS - 1:
-                    nc.sync.dma_start(out_rows[c][:, j, :], result[:, j, :])
-            if c < PAIRS - 1:
-                nc.sync.dma_start(out_rows[c], result[:])
+        def weigh(k):
+            h[k] = ring.tile([P, P, PACK], BF16, name="h", align_bytes=64)
+            nc.vector.tensor_tensor(h[k][:].rearrange("p (m i) t -> p m t i", i=4),
+                                    tanhs[k][:].rearrange("p t (m i) -> p m t i", i=4),
+                                    factor[:, :, k * P : (k + 1) * P].rearrange("p t (m i) -> p m t i", i=4), MULT)
 
-        def prepare(c):
-            load_rows(c)
-            interleave_x(c)
-            quantize_x(c)
-            scores(c)
-            turn_targets(c)
+        def quantize_h(k):
+            h_codes = ring.tile([P, P], U32, name="h_codes", align_bytes=64)
+            h_scales = ring.tile([P, P], U8, name="h_scales", align_bytes=64)
+            nc.vector.quantize_mx(out=h_codes[:].bitcast(E5M2), scales=h_scales[:],
+                                  in_=h[k][:].rearrange("p n t -> p (n t)"))
+            h_ops[k] = (h_codes, h_scales)
 
-        prepare(0)
-        turn_plane(PACK - 1)
-        residuals(0)
-        quantize_plane(PACK - 1)
-        for c in range(PAIRS):
-            if c + 1 < PAIRS:
-                prepare(c + 1)
-                residuals(c + 1)
-            weigh(c)
-            gradient(c)
+        def gradient(k):
+            h_codes, h_scales = h_ops[k]
+            grad = psum.tile([P, D], F32, name="grad", tag="o", bufs=3)
+            nc.tensor.matmul_mx(out=grad[:], lhsT=h_codes[:].bitcast(E5M2), lhsT_scale=h_scales[:],
+                                rhs=wi_codes[:].bitcast(E4M3), rhs_scale=wi_scales[:], start=True, stop=True)
+            result = ring.tile([P, D], F32, name="result", bufs=8)
+            natural = result[:].rearrange("r (p t) -> r p t", t=PACK)
+            planes = grad[:].rearrange("r (t p) -> r p t", t=PACK)
+            if k in [7]:
+                nc.vector.tensor_copy(natural, planes)
+            else:
+                nc.scalar.copy(natural, planes)
+            nc.sync.dma_start(out_rows[k], result[:])
+
+        stages = {"j": interleave_x, "w": quantize_x, "m": scores, "y": turn_targets, "B": scale_scores,
+                  "U": residual, "D": weigh, "q": quantize_h, "G": gradient, "t": turn_plane, "p": quantize_plane}
+        for item in ORDER:
+            stages[item[0]](int(item[1]))

@@ -16,13 +16,17 @@ E4M3 = mybir.dt.float8_e4m3fn_x4
 E5M2 = mybir.dt.float8_e5m2_x4
 ACT = mybir.ActivationFunctionType
 MULT = mybir.AluOpType.mult
+ADD = mybir.AluOpType.add
 
 P = 128
 PACK = 4
 PAIR = 2
+QUAD = 4
 CHUNKS = R // P
-LOADS = "x0 y0 x1 x2 y1 x3 y2 y3".split()
-ORDER = "j0 w0 j1 w1 m0 p1 p2 j2 y0 t3 B0 w2 U0 p3 m1 j3 y1 B1 w3 U1 m2 j4 y2 B2 w4 U2 m3 D0 j5 y3 B3 w5 q0 U3 m4 D1 j6 y4 B4 w6 q1 U4 m5 D2 j7 G0 y5 B5 w7 q2 U5 m6 D3 G1 y6 B6 q3 U6 m7 D4 G2 y7 B7 q4 U7 D5 G3 q5 D6 G4 q6 D7 G5 q7 G6 G7".split()
+LAG = 3
+BANK = 2048
+SLOT = 4 * T
+STEPPED = (0, CHUNKS - 1)
 
 
 def tile_attend_glch_x_ts_kernel(tc, xT, wT, y, wt, ts, offs, out):
@@ -30,24 +34,34 @@ def tile_attend_glch_x_ts_kernel(tc, xT, wT, y, wt, ts, offs, out):
     with ExitStack() as ctx:
         keep = ctx.enter_context(tc.tile_pool(name="keep", bufs=1))
         ring = ctx.enter_context(tc.tile_pool(name="ring", bufs=4))
+        stage = ctx.enter_context(tc.tile_pool(name="stage", bufs=1))
+        dealt = ctx.enter_context(tc.tile_pool(name="dealt", bufs=1))
         psum = ctx.enter_context(tc.psum_pool(name="psum", bufs=1))
 
-        offsets = keep.tile([P, N // 16], U16, name="offsets")
-        nc.sync.dma_start(offsets[:], offs)
-        wt_sb = keep.tile([P, R // P], F32, name="wt_sb")
-        nc.sync.dma_start(wt_sb[:], wt[0].rearrange("(p k) o -> p (k o)", p=P))
         w_rows = wT.rearrange("(p t) c -> t p c", t=PACK)
-        w_plane = [ring.tile([P, T], F32, name="w_plane%d" % t, tag="stage") for t in range(PACK)]
-        for t in range(PACK):
-            nc.sync.dma_start(w_plane[t][:], w_rows[t])
         x_rows = xT[0].rearrange("(p t) r -> p t r", t=PACK)
         y_rows = y[0].rearrange("(c j p) i -> c p j i", p=P, j=PAIR)
         out_rows = out[0].rearrange("(k p) d -> k p d", p=P)
 
-        ts_row = keep.tile([1, T], F32, name="ts_row")
-        nc.scalar.dma_start(ts_row[:], ts[0:1, :])
-        ts_window = keep.tile([P, T], F32, name="ts_window", tag="listed", align_bytes=64)
-        nc.vector.memset(ts_window[:], 0.0)
+        ts_row = keep.tile([1, T], F32, name="ts_row", tag="listed", align_bytes=64)
+        nc.sync.dma_start(ts_row[:], ts[0:1, :])
+        wt_sb = keep.tile([P, R // P], F32, name="wt_sb")
+        nc.sync.dma_start(wt_sb[:], wt[0].rearrange("(p k) o -> p (k o)", p=P))
+        offsets = keep.tile([P, N // 16], U16, name="offsets")
+        nc.sync.dma_start(offsets[:], offs)
+
+        ts_window = stage.tile([P, T], F32, name="ts_window", offset=(PACK - 1) * SLOT)
+        w_plane = {}
+
+        def load_plane(t):
+            w_plane[t] = stage.tile([P, T], F32, name="w_plane%d" % t, offset=t * SLOT)
+            nc.sync.dma_start(w_plane[t][:], w_rows[t])
+
+        for t in range(PACK - 1):
+            load_plane(t)
+
+        nc.vector.memset(ts_window[:, 0 : T // 2], 0.0)
+        nc.gpsimd.memset(ts_window[:, T // 2 : T], 0.0)
         nc.vector.tensor_copy(ts_window[0:1, :], ts_row[:])
 
         ident = keep.tile([P, P], F32, name="ident")
@@ -59,151 +73,225 @@ def tile_attend_glch_x_ts_kernel(tc, xT, wT, y, wt, ts, offs, out):
 
         ts_listed = keep.tile([P, N], F32, name="ts_listed")
         nc.vector.tensor_copy(ts_listed[:], ts_window[:].indirect(offsets[:]))
-        ts_turned = psum.tile([P, PACK, P], F32, name="ts_turned", tag="a", bufs=3)
+        load_plane(PACK - 1)
+
+        wt_row = keep.tile([P, R], F32, name="wt_row")
+        for half in range(2):
+            wt_spread = psum.tile([P, 4, P], F32, name="wt_spread%d" % half, offset=(2 + half) * BANK)
+            for k in range(4):
+                col = 4 * half + k
+                nc.tensor.transpose(wt_spread[:, k, :], wt_sb[:, col : col + 1].to_broadcast([P, P]), ident[:])
+            nc.scalar.copy(wt_row[:].rearrange("p (n k) -> p n k", k=8)[:, :, 4 * half : 4 * half + 4],
+                           wt_spread[:].rearrange("p k n -> p n k"))
+
+        ts_turned = psum.tile([P, PACK, P], F32, name="ts_turned", offset=5 * BANK)
         for t in range(PACK):
             nc.tensor.transpose(ts_turned[:, t, :], ts_listed[:, t::PACK], ident[:])
         ts_part = keep.tile([P, PACK], F32, name="ts_part")
         nc.scalar.copy(ts_part[:], ts_turned[:, :, 0])
-        ts_spread = psum.tile([P, PACK, P], F32, name="ts_spread", tag="a", bufs=3)
+        ts_spread = psum.tile([P, PACK, P], F32, name="ts_spread", offset=6 * BANK)
         for t in range(PACK):
             nc.tensor.transpose(ts_spread[:, t, :], ts_part[:, t : t + 1].to_broadcast([P, P]), ident[:])
         neg_ts = keep.tile([P, PACK, P], F32, name="neg_ts")
-        nc.scalar.activation(neg_ts[:], ts_spread[:], ACT.Copy, scale=-1.0)
+        factor = [keep.tile([P, PACK, R // 2], F32, name="factor%d" % half) for half in range(2)]
 
-        factor = keep.tile([P, PACK, R], F32, name="factor")
-        for half in range(2):
-            wt_spread = psum.tile([P, 4, P], F32, name="wt_spread", tag="z", bufs=2)
-            for k in range(4):
-                col = 4 * half + k
-                nc.tensor.transpose(wt_spread[:, k, :], wt_sb[:, col : col + 1].to_broadcast([P, P]), ident[:])
-            for t in range(PACK):
-                nc.scalar.activation(factor[:, t, :].rearrange("p (n k) -> p n k", k=8)[:, :, 4 * half : 4 * half + 4],
-                                     wt_spread[:].rearrange("p k n -> p n k"), ACT.Copy, scale=ts_part[:, t : t + 1])
+        def factor_on_scalar(t):
+            nc.scalar.activation(factor[0][:, t, :], wt_row[:, 0 : R // 2], ACT.Copy, scale=ts_part[:, t : t + 1])
 
-        w_listed = keep.tile([P, N, PACK], BF16, name="w_listed", tag="listed", align_bytes=64)
-        w_turned = keep.tile([P, PACK, P, PACK], BF16, name="w_turned", align_bytes=64)
+        for t in range(PACK):
+            nc.gpsimd.tensor_scalar(factor[1][:, t, :], wt_row[:, R // 2 : R], ts_part[:, t : t + 1], 0.0, MULT, ADD)
+
+        w_listed = keep.tile([P, PACK, P, PACK], BF16, name="w_listed", align_bytes=64)
         wd_codes = keep.tile([P, N], U32, name="wd_codes", align_bytes=64)
         wd_scales = keep.tile([P, N], U8, name="wd_scales", align_bytes=64)
         wi_codes = keep.tile([P, D], U32, name="wi_codes", align_bytes=64)
         wi_scales = keep.tile([P, D], U8, name="wi_scales", align_bytes=64)
+        w_turned = [keep.tile([P, PAIR, P, PACK], BF16, name="w_turned%d" % u, align_bytes=64) for u in range(PAIR)]
 
-        def gather_plane(t):
-            nc.vector.tensor_copy(w_listed[:, :, t], w_plane[t][:].indirect(offsets[:]))
+        early = keep.tile([P, (PACK - 1) * N], BF16, name="early", tag="listed", align_bytes=64)
 
-        def turn_plane(t):
-            if t == 2:
-                bank = psum.tile([P, PACK, P], BF16, name="w_bank", tag="a", bufs=3)
-            else:
-                bank = psum.tile([P, PACK, P], BF16, name="w_bank", tag="o", bufs=3)
+        def gather_early(t):
+            nc.vector.tensor_copy(early[:, t * N : (t + 1) * N], w_plane[t][:].indirect(offsets[:]))
+
+        def turn_early(t):
+            bank = psum.tile([P, PAIR, P], F32, name="w_bank%d" % t, offset=(5 + t) * BANK)
+            words = early[:, t * N : (t + 1) * N].bitcast(F32)
+            for u in range(PAIR):
+                nc.tensor.transpose(bank[:, u, :], words[:, u::PAIR], ident[:])
+            nc.scalar.copy(w_turned[t // PAIR][:, t % PAIR].rearrange("q p s -> q (p s)").bitcast(F32).rearrange("q (p u) -> q p u", u=PAIR),
+                           bank[:].rearrange("q u p -> q p u"))
+
+        def merge_early():
+            nc.vector.tensor_copy(w_listed[:, :, :, 0 : PACK - 1].rearrange("p s q t -> p q t s"),
+                                  early[:].rearrange("p (t q s) -> p q t s", t=PACK - 1, s=PACK))
+
+        def gather_last():
+            nc.vector.tensor_copy(w_listed[:, :, :, PACK - 1].rearrange("p s q -> p q s"), w_plane[PACK - 1][:].indirect(offsets[:]))
+
+        def turn_last():
+            bank = psum.tile([P, PACK, P], BF16, name="w_bank_last", offset=5 * BANK)
             for s in range(PACK):
-                nc.tensor.transpose(bank[:, s, :], w_listed[:, s::PACK, t], ident_bf[:])
-            if t in [0]:
-                nc.vector.tensor_copy(w_turned[:, t], bank[:].rearrange("q s p -> q p s"))
-            else:
-                nc.scalar.copy(w_turned[:, t], bank[:].rearrange("q s p -> q p s"))
+                nc.tensor.transpose(bank[:, s, :], w_listed[:, s, :, PACK - 1], ident_bf[:])
+            nc.scalar.copy(w_turned[1][:, 1], bank[:].rearrange("q s p -> q p s"))
 
-        def quantize_plane(t):
-            nc.vector.quantize_mx(out=wi_codes[:, t * P : (t + 1) * P].bitcast(E4M3),
-                                  scales=wi_scales[:, t * P : (t + 1) * P],
-                                  in_=w_turned[:, t].rearrange("q p s -> q (p s)"))
-
-        gather_plane(0)
-        gather_plane(1)
-        turn_plane(0)
-        gather_plane(2)
-        turn_plane(1)
-        gather_plane(3)
-        turn_plane(2)
-        quantize_plane(0)
-        nc.vector.quantize_mx(out=wd_codes[:].bitcast(E4M3), scales=wd_scales[:],
-                              in_=w_listed[:].rearrange("p i t -> p (i t)"))
+        def quantize_planes(u):
+            cols = slice(u * PAIR * P, (u + 1) * PAIR * P)
+            nc.vector.quantize_mx(out=wi_codes[:, cols].bitcast(E4M3), scales=wi_scales[:, cols],
+                                  in_=w_turned[u][:].rearrange("q t p s -> q (t p s)"))
 
         x_raw = {}
         y_sb = {}
-        for item in LOADS:
-            c = int(item[1])
-            if item[0] == "x":
-                x_raw[c] = ring.tile([P, PACK, P * PAIR], F32, name="x_raw", tag="stage")
-                nc.sync.dma_start(x_raw[c][:], x_rows[:, :, c * P * PAIR : (c + 1) * P * PAIR])
-            else:
-                y_sb[c] = ring.tile([P, PAIR, N], F32, name="y_sb", tag="stage")
-                nc.sync.dma_start(y_sb[c][:], y_rows[c])
 
-        x_codes = keep.tile([P, R], U32, name="x_codes", align_bytes=64)
-        x_scales = keep.tile([P, R], U8, name="x_scales", align_bytes=64)
+        def load_pairs(slot, first, second):
+            both = stage.tile([P, T], F32, name="pairs%d" % slot, offset=slot * SLOT)
+            for c, (name, pair) in enumerate([first, second]):
+                half = both[:, c * T // 2 : (c + 1) * T // 2]
+                if name == "x":
+                    x_raw[pair] = half.rearrange("p (t r) -> p t r", t=PACK)
+                    nc.sync.dma_start(x_raw[pair], x_rows[:, :, pair * P * PAIR : (pair + 1) * P * PAIR])
+                else:
+                    y_sb[pair] = half.rearrange("p (j i) -> p j i", j=PAIR)
+                    nc.sync.dma_start(y_sb[pair], y_rows[pair])
+
+        gather_early(0)
+        load_pairs(0, ("x", 0), ("x", 1))
+        turn_early(0)
+        nc.scalar.activation(neg_ts[:], ts_spread[:], ACT.Copy, scale=-1.0)
+        factor_on_scalar(0)
+        factor_on_scalar(1)
+        gather_early(1)
+        load_pairs(1, ("y", 0), ("y", 1))
+        turn_early(1)
+        factor_on_scalar(2)
+        factor_on_scalar(3)
+        gather_early(2)
+        load_pairs(2, ("x", 2), ("y", 2))
+        quantize_planes(0)
+        turn_early(2)
+        merge_early()
+        gather_last()
+        load_pairs(3, ("x", 3), ("y", 3))
+        nc.vector.quantize_mx(out=wd_codes[:].bitcast(E4M3), scales=wd_scales[:],
+                              in_=w_listed[:].rearrange("p s q t -> p (s q t)"))
+
         x_grouped = {}
+        x_ops = {}
         sums = {}
+        y_dealt = {}
         targets = {}
         neg_a = {}
         tanhs = {}
         h = {}
         h_ops = {}
+        grads = {}
 
         def interleave_x(k):
-            x_grouped[k] = ring.tile([P, P, PACK], BF16, name="x_grouped", align_bytes=64, bufs=6)
+            if k == 0:
+                x_grouped[k] = keep.tile([P, P, PACK], BF16, name="x_grouped_first", align_bytes=64)
+            else:
+                x_grouped[k] = ring.tile([P, P, PACK], BF16, name="x_grouped", align_bytes=64, bufs=1)
             dst = x_grouped[k][:].rearrange("p (m i) t -> p m t i", i=4)
             src = x_raw[k // PAIR][:, :, (k % PAIR) * P : (k % PAIR + 1) * P].rearrange("p t (m i) -> p m t i", i=4)
-            if k in []:
-                nc.vector.tensor_copy(dst, src)
-            else:
-                nc.scalar.copy(dst, src)
+            nc.scalar.copy(dst, src)
 
         def quantize_x(k):
-            cols = slice(k * P, (k + 1) * P)
-            nc.vector.quantize_mx(out=x_codes[:, cols].bitcast(E4M3), scales=x_scales[:, cols],
+            if k == 0:
+                x_codes = dealt.tile([P, P], U32, name="x_codes_first", align_bytes=64, offset=4 * N)
+            else:
+                x_codes = ring.tile([P, P], U32, name="x_codes", align_bytes=64, bufs=1)
+            x_scales = ring.tile([P, P], U8, name="x_scales", align_bytes=64, bufs=2)
+            nc.vector.quantize_mx(out=x_codes[:].bitcast(E4M3), scales=x_scales[:],
                                   in_=x_grouped[k][:].rearrange("p n t -> p (n t)"))
+            x_ops[k] = (x_codes, x_scales)
 
         def scores(k):
-            cols = slice(k * P, (k + 1) * P)
-            sums[k] = psum.tile([P, N], F32, name="a", tag="a", bufs=3)
-            nc.tensor.matmul_mx(out=sums[k][:], lhsT=x_codes[:, cols].bitcast(E4M3), lhsT_scale=x_scales[:, cols],
+            x_codes, x_scales = x_ops[k]
+            sums[k] = psum.tile([P, N], F32, name="a%d" % k, offset=(k % 2) * BANK)
+            nc.tensor.matmul_mx(out=sums[k][:], lhsT=x_codes[:].bitcast(E4M3), lhsT_scale=x_scales[:],
                                 rhs=wd_codes[:].bitcast(E4M3), rhs_scale=wd_scales[:], start=True, stop=True)
 
-        def turn_targets(k):
-            targets[k] = psum.tile([P, PACK, P], F32, name="z", tag="z", bufs=2)
-            for t in range(PACK):
-                nc.tensor.matmul(targets[k][:, t, :], y_sb[k // PAIR][:, k % PAIR, t::PACK], ident[:],
-                                 start=(t == 0), stop=False, is_transpose=True)
+        def deal_targets(k):
+            y_dealt[k] = dealt.tile([P, PACK, P], F32, name="y_dealt%d" % k, align_bytes=64, offset=(k % 2) * 4 * N)
+            nc.vector.tensor_copy(y_dealt[k][:].rearrange("r t (m i) -> r m t i", i=4),
+                                  y_sb[k // PAIR][:, k % PAIR, :].rearrange("r (m i t) -> r m t i", i=4, t=PACK))
 
         def scale_scores(k):
-            neg_a[k] = ring.tile([P, PACK, P], F32, name="neg_a")
-            nc.vector.tensor_tensor(neg_a[k][:], sums[k][:].rearrange("r (p t) -> r t p", t=PACK), neg_ts[:], MULT)
+            if k == 0:
+                neg_a[k] = dealt.tile([P, N], F32, name="neg_a_first", align_bytes=64, offset=0)
+            else:
+                neg_a[k] = ring.tile([P, N], F32, name="neg_a", bufs=2)
+            nc.vector.tensor_tensor(neg_a[k][:], sums[k][:], neg_ts[:].rearrange("r t p -> r (t p)"), MULT)
 
         def residual(k):
-            for t in range(PACK):
-                nc.tensor.matmul(targets[k][:, t, :], neg_a[k][:, t, :], ident[:], start=False,
-                                 stop=(t == PACK - 1), is_transpose=True)
-            tanhs[k] = ring.tile([P, PACK, P], F32, name="tanh")
+            scored = [neg_a[k][:, t * P : (t + 1) * P] for t in range(PACK)]
+            if k in STEPPED:
+                wanted = [y_sb[k // PAIR][:, k % PAIR, t::PACK] for t in range(PACK)]
+            else:
+                wanted = [y_dealt[k][:, t, :] for t in range(PACK)]
+            terms = wanted + scored if k == CHUNKS - 1 else scored + wanted
+            targets[k] = psum.tile([P, PACK, P], F32, name="z%d" % k, offset=(2 + k % 3) * BANK)
+            for n, term in enumerate(terms):
+                nc.tensor.matmul(targets[k][:, n % PACK, :], term, ident[:], start=(n == 0),
+                                 stop=(n == len(terms) - 1), is_transpose=True)
+
+        def squash(k):
+            tanhs[k] = ring.tile([P, PACK, P], F32, name="tanh", bufs=LAG + 1)
             nc.scalar.activation(tanhs[k][:], targets[k][:], ACT.Tanh, scale=-1.0)
 
         def weigh(k):
-            h[k] = ring.tile([P, P, PACK], BF16, name="h", align_bytes=64)
+            h[k] = ring.tile([P, P, PACK], BF16, name="h", align_bytes=64, bufs=2)
+            rows = slice((k % QUAD) * P, (k % QUAD + 1) * P)
             nc.vector.tensor_tensor(h[k][:].rearrange("p (m i) t -> p m t i", i=4),
                                     tanhs[k][:].rearrange("p t (m i) -> p m t i", i=4),
-                                    factor[:, :, k * P : (k + 1) * P].rearrange("p t (m i) -> p m t i", i=4), MULT)
+                                    factor[k // QUAD][:, :, rows].rearrange("p t (m i) -> p m t i", i=4), MULT)
 
         def quantize_h(k):
-            h_codes = ring.tile([P, P], U32, name="h_codes", align_bytes=64)
-            h_scales = ring.tile([P, P], U8, name="h_scales", align_bytes=64)
+            h_codes = ring.tile([P, P], U32, name="h_codes", align_bytes=64, bufs=2)
+            h_scales = ring.tile([P, P], U8, name="h_scales", align_bytes=64, bufs=2)
             nc.vector.quantize_mx(out=h_codes[:].bitcast(E5M2), scales=h_scales[:],
                                   in_=h[k][:].rearrange("p n t -> p (n t)"))
             h_ops[k] = (h_codes, h_scales)
 
         def gradient(k):
             h_codes, h_scales = h_ops[k]
-            grad = psum.tile([P, D], F32, name="grad", tag="o", bufs=3)
-            nc.tensor.matmul_mx(out=grad[:], lhsT=h_codes[:].bitcast(E5M2), lhsT_scale=h_scales[:],
+            grads[k] = psum.tile([P, D], F32, name="grad%d" % k, offset=(5 + (k + 1) % 3) * BANK)
+            nc.tensor.matmul_mx(out=grads[k][:], lhsT=h_codes[:].bitcast(E5M2), lhsT_scale=h_scales[:],
                                 rhs=wi_codes[:].bitcast(E4M3), rhs_scale=wi_scales[:], start=True, stop=True)
-            result = ring.tile([P, D], F32, name="result", bufs=8)
+
+        def store(k):
+            result = ring.tile([P, D], F32, name="result", bufs=CHUNKS)
             natural = result[:].rearrange("r (p t) -> r p t", t=PACK)
-            planes = grad[:].rearrange("r (t p) -> r p t", t=PACK)
-            if k in [7]:
+            planes = grads[k][:].rearrange("r (t p) -> r p t", t=PACK)
+            if k == CHUNKS - 1:
                 nc.vector.tensor_copy(natural, planes)
             else:
                 nc.scalar.copy(natural, planes)
             nc.sync.dma_start(out_rows[k], result[:])
 
-        stages = {"j": interleave_x, "w": quantize_x, "m": scores, "y": turn_targets, "B": scale_scores,
-                  "U": residual, "D": weigh, "q": quantize_h, "G": gradient, "t": turn_plane, "p": quantize_plane}
-        for item in ORDER:
-            stages[item[0]](int(item[1]))
+        def each(stage, k):
+            if 0 <= k < CHUNKS:
+                stage(k)
+
+        interleave_x(0)
+        interleave_x(1)
+        quantize_x(0)
+        quantize_x(1)
+        scores(0)
+        scores(1)
+        turn_last()
+        interleave_x(2)
+        for s in range(CHUNKS + LAG):
+            each(scale_scores, s)
+            each(residual, s)
+            each(quantize_x, s + 2)
+            each(scores, s + 2)
+            each(weigh, s - LAG)
+            if s + 1 not in STEPPED:
+                each(deal_targets, s + 1)
+            if s == 0:
+                quantize_planes(1)
+            each(quantize_h, s - LAG)
+            each(gradient, s - LAG)
+            each(squash, s)
+            each(interleave_x, s + 3)
+            each(store, s - LAG)

@@ -26,7 +26,7 @@ CHUNKS = R // P
 LAG = 3
 BANK = 2048
 SLOT = 4 * T
-STEPPED = (0, CHUNKS - 1)
+STEPPED = (0, 2, 4, 6, 7)
 
 
 def tile_attend_glch_x_ts_kernel(tc, xT, wT, y, wt, ts, offs, out):
@@ -68,8 +68,6 @@ def tile_attend_glch_x_ts_kernel(tc, xT, wT, y, wt, ts, offs, out):
         make_identity(nc, ident[:])
         warm = keep.tile([P, 1], F32, name="warm")
         nc.scalar.activation(warm[:], ident[:, 0:1], ACT.Tanh)
-        ident_bf = keep.tile([P, P], BF16, name="ident_bf")
-        make_identity(nc, ident_bf[:])
 
         ts_listed = keep.tile([P, N], F32, name="ts_listed")
         nc.vector.tensor_copy(ts_listed[:], ts_window[:].indirect(offsets[:]))
@@ -101,38 +99,29 @@ def tile_attend_glch_x_ts_kernel(tc, xT, wT, y, wt, ts, offs, out):
         for t in range(PACK):
             nc.gpsimd.tensor_scalar(factor[1][:, t, :], wt_row[:, R // 2 : R], ts_part[:, t : t + 1], 0.0, MULT, ADD)
 
-        w_listed = keep.tile([P, PACK, P, PACK], BF16, name="w_listed", align_bytes=64)
+        w_listed = keep.tile([P, N, PACK], BF16, name="w_listed", align_bytes=64)
         wd_codes = keep.tile([P, N], U32, name="wd_codes", align_bytes=64)
         wd_scales = keep.tile([P, N], U8, name="wd_scales", align_bytes=64)
         wi_codes = keep.tile([P, D], U32, name="wi_codes", align_bytes=64)
         wi_scales = keep.tile([P, D], U8, name="wi_scales", align_bytes=64)
         w_turned = [keep.tile([P, PAIR, P, PACK], BF16, name="w_turned%d" % u, align_bytes=64) for u in range(PAIR)]
 
-        early = keep.tile([P, (PACK - 1) * N], BF16, name="early", tag="listed", align_bytes=64)
+        planes = keep.tile([P, PACK * N], BF16, name="planes", tag="listed", align_bytes=64)
 
-        def gather_early(t):
-            nc.vector.tensor_copy(early[:, t * N : (t + 1) * N], w_plane[t][:].indirect(offsets[:]))
+        def gather_plane(t):
+            nc.vector.tensor_copy(planes[:, t * N : (t + 1) * N], w_plane[t][:].indirect(offsets[:]))
 
-        def turn_early(t):
-            bank = psum.tile([P, PAIR, P], F32, name="w_bank%d" % t, offset=(5 + t) * BANK)
-            words = early[:, t * N : (t + 1) * N].bitcast(F32)
+        def turn_plane(t):
+            bank = psum.tile([P, PAIR, P], F32, name="w_bank%d" % t, offset=(5 + t % 3) * BANK)
+            words = planes[:, t * N : (t + 1) * N].bitcast(F32)
             for u in range(PAIR):
                 nc.tensor.transpose(bank[:, u, :], words[:, u::PAIR], ident[:])
             nc.scalar.copy(w_turned[t // PAIR][:, t % PAIR].rearrange("q p s -> q (p s)").bitcast(F32).rearrange("q (p u) -> q p u", u=PAIR),
                            bank[:].rearrange("q u p -> q p u"))
 
-        def merge_early():
-            nc.vector.tensor_copy(w_listed[:, :, :, 0 : PACK - 1].rearrange("p s q t -> p q t s"),
-                                  early[:].rearrange("p (t q s) -> p q t s", t=PACK - 1, s=PACK))
-
-        def gather_last():
-            nc.vector.tensor_copy(w_listed[:, :, :, PACK - 1].rearrange("p s q -> p q s"), w_plane[PACK - 1][:].indirect(offsets[:]))
-
-        def turn_last():
-            bank = psum.tile([P, PACK, P], BF16, name="w_bank_last", offset=5 * BANK)
-            for s in range(PACK):
-                nc.tensor.transpose(bank[:, s, :], w_listed[:, s, :, PACK - 1], ident_bf[:])
-            nc.scalar.copy(w_turned[1][:, 1], bank[:].rearrange("q s p -> q p s"))
+        def interleave_planes():
+            nc.vector.tensor_copy(w_listed[:].rearrange("p (m i) t -> p m t i", i=4),
+                                  planes[:].rearrange("p (t m i) -> p m t i", t=PACK, i=4))
 
         def quantize_planes(u):
             cols = slice(u * PAIR * P, (u + 1) * PAIR * P)
@@ -153,26 +142,26 @@ def tile_attend_glch_x_ts_kernel(tc, xT, wT, y, wt, ts, offs, out):
                     y_sb[pair] = half.rearrange("p (j i) -> p j i", j=PAIR)
                     nc.sync.dma_start(y_sb[pair], y_rows[pair])
 
-        gather_early(0)
+        gather_plane(0)
         load_pairs(0, ("x", 0), ("x", 1))
-        turn_early(0)
+        turn_plane(0)
         nc.scalar.activation(neg_ts[:], ts_spread[:], ACT.Copy, scale=-1.0)
         factor_on_scalar(0)
         factor_on_scalar(1)
-        gather_early(1)
+        gather_plane(1)
         load_pairs(1, ("y", 0), ("y", 1))
-        turn_early(1)
+        turn_plane(1)
         factor_on_scalar(2)
         factor_on_scalar(3)
-        gather_early(2)
+        gather_plane(2)
         load_pairs(2, ("x", 2), ("y", 2))
         quantize_planes(0)
-        turn_early(2)
-        merge_early()
-        gather_last()
+        turn_plane(2)
+        gather_plane(3)
         load_pairs(3, ("x", 3), ("y", 3))
+        interleave_planes()
         nc.vector.quantize_mx(out=wd_codes[:].bitcast(E4M3), scales=wd_scales[:],
-                              in_=w_listed[:].rearrange("p s q t -> p (s q t)"))
+                              in_=w_listed[:].rearrange("p i t -> p (i t)"))
 
         x_grouped = {}
         x_ops = {}
@@ -216,11 +205,8 @@ def tile_attend_glch_x_ts_kernel(tc, xT, wT, y, wt, ts, offs, out):
                                   y_sb[k // PAIR][:, k % PAIR, :].rearrange("r (m i t) -> r m t i", i=4, t=PACK))
 
         def scale_scores(k):
-            if k == 0:
-                neg_a[k] = dealt.tile([P, N], F32, name="neg_a_first", align_bytes=64, offset=0)
-            else:
-                neg_a[k] = ring.tile([P, N], F32, name="neg_a", bufs=2)
-            nc.vector.tensor_tensor(neg_a[k][:], sums[k][:], neg_ts[:].rearrange("r t p -> r (t p)"), MULT)
+            neg_a[k] = ring.tile([P, N], F32, name="neg_a", bufs=2)
+            nc.vector.tensor_tensor(neg_a[k][:].rearrange("r (t p) -> r t p", t=PACK), sums[k][:].rearrange("r (p t) -> r t p", t=PACK), neg_ts[:], MULT)
 
         def residual(k):
             scored = [neg_a[k][:, t * P : (t + 1) * P] for t in range(PACK)]
@@ -278,7 +264,7 @@ def tile_attend_glch_x_ts_kernel(tc, xT, wT, y, wt, ts, offs, out):
         quantize_x(1)
         scores(0)
         scores(1)
-        turn_last()
+        turn_plane(PACK - 1)
         interleave_x(2)
         for s in range(CHUNKS + LAG):
             each(scale_scores, s)

@@ -23,10 +23,12 @@ PACK = 4
 PAIR = 2
 QUAD = 4
 CHUNKS = R // P
-LAG = 3
+LAG = 2
 BANK = 2048
 SLOT = 4 * T
-STEPPED = (0, 2, 4, 6, 7)
+STEPPED = (0, 4, 7)
+WARM_SCORES = (1, 3)
+WARM_GRADIENT = (4, 5)
 
 
 def tile_attend_glch_x_ts_kernel(tc, xT, wT, y, wt, ts, offs, out):
@@ -163,6 +165,7 @@ def tile_attend_glch_x_ts_kernel(tc, xT, wT, y, wt, ts, offs, out):
         nc.vector.quantize_mx(out=wd_codes[:].bitcast(E4M3), scales=wd_scales[:],
                               in_=w_listed[:].rearrange("p i t -> p (i t)"))
 
+        unread = psum.tile([P, N], F32, name="unread", offset=4 * BANK)
         x_grouped = {}
         x_ops = {}
         sums = {}
@@ -179,8 +182,8 @@ def tile_attend_glch_x_ts_kernel(tc, xT, wT, y, wt, ts, offs, out):
                 x_grouped[k] = keep.tile([P, P, PACK], BF16, name="x_grouped_first", align_bytes=64)
             else:
                 x_grouped[k] = ring.tile([P, P, PACK], BF16, name="x_grouped", align_bytes=64, bufs=1)
-            dst = x_grouped[k][:].rearrange("p (m i) t -> p m t i", i=4)
-            src = x_raw[k // PAIR][:, :, (k % PAIR) * P : (k % PAIR + 1) * P].rearrange("p t (m i) -> p m t i", i=4)
+            dst = x_grouped[k][:].rearrange("p (m i) t -> p m t i", i=PAIR)
+            src = x_raw[k // PAIR][:, :, (k % PAIR) * P : (k % PAIR + 1) * P].rearrange("p t (m i) -> p m t i", i=PAIR)
             nc.scalar.copy(dst, src)
 
         def quantize_x(k):
@@ -198,14 +201,20 @@ def tile_attend_glch_x_ts_kernel(tc, xT, wT, y, wt, ts, offs, out):
             sums[k] = psum.tile([P, N], F32, name="a%d" % k, offset=(k % 2) * BANK)
             nc.tensor.matmul_mx(out=sums[k][:], lhsT=x_codes[:].bitcast(E4M3), lhsT_scale=x_scales[:],
                                 rhs=wd_codes[:].bitcast(E4M3), rhs_scale=wd_scales[:], start=True, stop=True)
+            if k in WARM_SCORES:
+                nc.tensor.matmul_mx(out=unread[:], lhsT=x_codes[:].bitcast(E4M3), lhsT_scale=x_scales[:],
+                                    rhs=wd_codes[:].bitcast(E4M3), rhs_scale=wd_scales[:], start=True, stop=True)
 
         def deal_targets(k):
             y_dealt[k] = dealt.tile([P, PACK, P], F32, name="y_dealt%d" % k, align_bytes=64, offset=(k % 2) * 4 * N)
-            nc.vector.tensor_copy(y_dealt[k][:].rearrange("r t (m i) -> r m t i", i=4),
-                                  y_sb[k // PAIR][:, k % PAIR, :].rearrange("r (m i t) -> r m t i", i=4, t=PACK))
+            nc.vector.tensor_copy(y_dealt[k][:].rearrange("r (u e) (m i) -> r m u i e", e=PAIR, i=4),
+                                  y_sb[k // PAIR][:, k % PAIR, :].rearrange("r (m i u e) -> r m u i e", i=4, u=PAIR, e=PAIR))
 
         def scale_scores(k):
-            neg_a[k] = ring.tile([P, N], F32, name="neg_a", bufs=2)
+            if k == 0:
+                neg_a[k] = dealt.tile([P, N], F32, name="neg_a_first", align_bytes=64, offset=0)
+            else:
+                neg_a[k] = ring.tile([P, N], F32, name="neg_a", bufs=2)
             nc.vector.tensor_tensor(neg_a[k][:].rearrange("r (t p) -> r t p", t=PACK), sums[k][:].rearrange("r (p t) -> r t p", t=PACK), neg_ts[:], MULT)
 
         def residual(k):
@@ -215,7 +224,7 @@ def tile_attend_glch_x_ts_kernel(tc, xT, wT, y, wt, ts, offs, out):
             else:
                 wanted = [y_dealt[k][:, t, :] for t in range(PACK)]
             terms = wanted + scored if k == CHUNKS - 1 else scored + wanted
-            targets[k] = psum.tile([P, PACK, P], F32, name="z%d" % k, offset=(2 + k % 3) * BANK)
+            targets[k] = psum.tile([P, PACK, P], F32, name="z%d" % k, offset=(2 + k % 2) * BANK)
             for n, term in enumerate(terms):
                 nc.tensor.matmul(targets[k][:, n % PACK, :], term, ident[:], start=(n == 0),
                                  stop=(n == len(terms) - 1), is_transpose=True)
@@ -227,9 +236,9 @@ def tile_attend_glch_x_ts_kernel(tc, xT, wT, y, wt, ts, offs, out):
         def weigh(k):
             h[k] = ring.tile([P, P, PACK], BF16, name="h", align_bytes=64, bufs=2)
             rows = slice((k % QUAD) * P, (k % QUAD + 1) * P)
-            nc.vector.tensor_tensor(h[k][:].rearrange("p (m i) t -> p m t i", i=4),
-                                    tanhs[k][:].rearrange("p t (m i) -> p m t i", i=4),
-                                    factor[k // QUAD][:, :, rows].rearrange("p t (m i) -> p m t i", i=4), MULT)
+            nc.vector.tensor_tensor(h[k][:].rearrange("p (m i) t -> p m t i", i=PAIR),
+                                    tanhs[k][:].rearrange("p t (m i) -> p m t i", i=PAIR),
+                                    factor[k // QUAD][:, :, rows].rearrange("p t (m i) -> p m t i", i=PAIR), MULT)
 
         def quantize_h(k):
             h_codes = ring.tile([P, P], U32, name="h_codes", align_bytes=64, bufs=2)
@@ -243,6 +252,9 @@ def tile_attend_glch_x_ts_kernel(tc, xT, wT, y, wt, ts, offs, out):
             grads[k] = psum.tile([P, D], F32, name="grad%d" % k, offset=(5 + (k + 1) % 3) * BANK)
             nc.tensor.matmul_mx(out=grads[k][:], lhsT=h_codes[:].bitcast(E5M2), lhsT_scale=h_scales[:],
                                 rhs=wi_codes[:].bitcast(E4M3), rhs_scale=wi_scales[:], start=True, stop=True)
+            if k in WARM_GRADIENT:
+                nc.tensor.matmul_mx(out=unread[:], lhsT=h_codes[:].bitcast(E5M2), lhsT_scale=h_scales[:],
+                                    rhs=wi_codes[:].bitcast(E4M3), rhs_scale=wi_scales[:], start=True, stop=True)
 
         def store(k):
             result = ring.tile([P, D], F32, name="result", bufs=CHUNKS)

@@ -23,12 +23,12 @@ PACK = 4
 PAIR = 2
 QUAD = 4
 CHUNKS = R // P
-LAG = 2
+LAG = 3
+HALF = 2 * T
 BANK = 2048
 SLOT = 4 * T
-STEPPED = (0, 4, 7)
-WARM_SCORES = (1, 3)
-WARM_GRADIENT = (4, 5)
+WARM_SCORES = (2, 4)
+WARM_GRADIENT = (3, 4)
 
 
 def tile_attend_glch_x_ts_kernel(tc, xT, wT, y, wt, ts, offs, out):
@@ -37,7 +37,6 @@ def tile_attend_glch_x_ts_kernel(tc, xT, wT, y, wt, ts, offs, out):
         keep = ctx.enter_context(tc.tile_pool(name="keep", bufs=1))
         ring = ctx.enter_context(tc.tile_pool(name="ring", bufs=4))
         stage = ctx.enter_context(tc.tile_pool(name="stage", bufs=1))
-        dealt = ctx.enter_context(tc.tile_pool(name="dealt", bufs=1))
         psum = ctx.enter_context(tc.psum_pool(name="psum", bufs=1))
 
         w_rows = wT.rearrange("(p t) c -> t p c", t=PACK)
@@ -45,18 +44,18 @@ def tile_attend_glch_x_ts_kernel(tc, xT, wT, y, wt, ts, offs, out):
         y_rows = y[0].rearrange("(c j p) i -> c p j i", p=P, j=PAIR)
         out_rows = out[0].rearrange("(k p) d -> k p d", p=P)
 
-        ts_row = keep.tile([1, T], F32, name="ts_row", tag="listed", align_bytes=64)
+        ts_row = stage.tile([1, T], F32, name="ts_row", align_bytes=64, offset=4 * SLOT)
         nc.sync.dma_start(ts_row[:], ts[0:1, :])
         wt_sb = keep.tile([P, R // P], F32, name="wt_sb")
         nc.sync.dma_start(wt_sb[:], wt[0].rearrange("(p k) o -> p (k o)", p=P))
         offsets = keep.tile([P, N // 16], U16, name="offsets")
         nc.sync.dma_start(offsets[:], offs)
 
-        ts_window = stage.tile([P, T], F32, name="ts_window", offset=(PACK - 1) * SLOT)
+        ts_window = stage.tile([P, T], F32, name="ts_window", align_bytes=64, offset=(PACK - 1) * SLOT)
         w_plane = {}
 
         def load_plane(t):
-            w_plane[t] = stage.tile([P, T], F32, name="w_plane%d" % t, offset=t * SLOT)
+            w_plane[t] = stage.tile([P, T], F32, name="w_plane%d" % t, align_bytes=64, offset=t * SLOT)
             nc.sync.dma_start(w_plane[t][:], w_rows[t])
 
         for t in range(PACK - 1):
@@ -101,14 +100,15 @@ def tile_attend_glch_x_ts_kernel(tc, xT, wT, y, wt, ts, offs, out):
         for t in range(PACK):
             nc.gpsimd.tensor_scalar(factor[1][:, t, :], wt_row[:, R // 2 : R], ts_part[:, t : t + 1], 0.0, MULT, ADD)
 
-        w_listed = keep.tile([P, N, PACK], BF16, name="w_listed", align_bytes=64)
+        w_listed = stage.tile([P, N, PACK], BF16, name="w_listed", align_bytes=64, offset=2 * SLOT + HALF)
         wd_codes = keep.tile([P, N], U32, name="wd_codes", align_bytes=64)
         wd_scales = keep.tile([P, N], U8, name="wd_scales", align_bytes=64)
         wi_codes = keep.tile([P, D], U32, name="wi_codes", align_bytes=64)
         wi_scales = keep.tile([P, D], U8, name="wi_scales", align_bytes=64)
-        w_turned = [keep.tile([P, PAIR, P, PACK], BF16, name="w_turned%d" % u, align_bytes=64) for u in range(PAIR)]
+        w_turned = [stage.tile([P, PAIR, P, PACK], BF16, name="w_turned0", align_bytes=64, offset=0),
+                    keep.tile([P, PAIR, P, PACK], BF16, name="w_turned1", align_bytes=64)]
 
-        planes = keep.tile([P, PACK * N], BF16, name="planes", tag="listed", align_bytes=64)
+        planes = stage.tile([P, PACK * N], BF16, name="planes", align_bytes=64, offset=4 * SLOT)
 
         def gather_plane(t):
             nc.vector.tensor_copy(planes[:, t * N : (t + 1) * N], w_plane[t][:].indirect(offsets[:]))
@@ -133,34 +133,32 @@ def tile_attend_glch_x_ts_kernel(tc, xT, wT, y, wt, ts, offs, out):
         x_raw = {}
         y_sb = {}
 
-        def load_pairs(slot, first, second):
-            both = stage.tile([P, T], F32, name="pairs%d" % slot, offset=slot * SLOT)
-            for c, (name, pair) in enumerate([first, second]):
-                half = both[:, c * T // 2 : (c + 1) * T // 2]
-                if name == "x":
-                    x_raw[pair] = half.rearrange("p (t r) -> p t r", t=PACK)
-                    nc.sync.dma_start(x_raw[pair], x_rows[:, :, pair * P * PAIR : (pair + 1) * P * PAIR])
-                else:
-                    y_sb[pair] = half.rearrange("p (j i) -> p j i", j=PAIR)
-                    nc.sync.dma_start(y_sb[pair], y_rows[pair])
+        def load_x(pair, offset):
+            x_raw[pair] = stage.tile([P, PACK, PAIR * P], F32, name="x_raw%d" % pair, align_bytes=64, offset=offset)
+            nc.sync.dma_start(x_raw[pair][:], x_rows[:, :, pair * P * PAIR : (pair + 1) * P * PAIR])
+
+        def load_y(pair, offset):
+            y_sb[pair] = stage.tile([P, PAIR, N], F32, name="y_sb%d" % pair, align_bytes=64, offset=offset)
+            nc.sync.dma_start(y_sb[pair][:], y_rows[pair])
 
         gather_plane(0)
-        load_pairs(0, ("x", 0), ("x", 1))
         turn_plane(0)
         nc.scalar.activation(neg_ts[:], ts_spread[:], ACT.Copy, scale=-1.0)
         factor_on_scalar(0)
         factor_on_scalar(1)
         gather_plane(1)
-        load_pairs(1, ("y", 0), ("y", 1))
+        load_y(0, SLOT)
+        load_x(0, SLOT + HALF)
         turn_plane(1)
         factor_on_scalar(2)
         factor_on_scalar(3)
         gather_plane(2)
-        load_pairs(2, ("x", 2), ("y", 2))
+        load_x(1, 2 * SLOT)
         quantize_planes(0)
+        load_y(1, 0)
         turn_plane(2)
         gather_plane(3)
-        load_pairs(3, ("x", 3), ("y", 3))
+        load_x(2, 3 * SLOT)
         interleave_planes()
         nc.vector.quantize_mx(out=wd_codes[:].bitcast(E4M3), scales=wd_scales[:],
                               in_=w_listed[:].rearrange("p i t -> p (i t)"))
@@ -169,7 +167,6 @@ def tile_attend_glch_x_ts_kernel(tc, xT, wT, y, wt, ts, offs, out):
         x_grouped = {}
         x_ops = {}
         sums = {}
-        y_dealt = {}
         targets = {}
         neg_a = {}
         tanhs = {}
@@ -178,20 +175,17 @@ def tile_attend_glch_x_ts_kernel(tc, xT, wT, y, wt, ts, offs, out):
         grads = {}
 
         def interleave_x(k):
-            if k == 0:
-                x_grouped[k] = keep.tile([P, P, PACK], BF16, name="x_grouped_first", align_bytes=64)
-            else:
-                x_grouped[k] = ring.tile([P, P, PACK], BF16, name="x_grouped", align_bytes=64, bufs=1)
+            x_grouped[k] = ring.tile([P, P, PACK], BF16, name="x_grouped", align_bytes=64, bufs=3)
             dst = x_grouped[k][:].rearrange("p (m i) t -> p m t i", i=PAIR)
             src = x_raw[k // PAIR][:, :, (k % PAIR) * P : (k % PAIR + 1) * P].rearrange("p t (m i) -> p m t i", i=PAIR)
             nc.scalar.copy(dst, src)
 
         def quantize_x(k):
             if k == 0:
-                x_codes = dealt.tile([P, P], U32, name="x_codes_first", align_bytes=64, offset=4 * N)
+                x_codes = stage.tile([P, P], U32, name="x_codes_first", align_bytes=64, offset=HALF)
             else:
-                x_codes = ring.tile([P, P], U32, name="x_codes", align_bytes=64, bufs=1)
-            x_scales = ring.tile([P, P], U8, name="x_scales", align_bytes=64, bufs=2)
+                x_codes = ring.tile([P, P], U32, name="x_codes", align_bytes=64, bufs=2)
+            x_scales = ring.tile([P, P], U8, name="x_scales", align_bytes=64, bufs=3)
             nc.vector.quantize_mx(out=x_codes[:].bitcast(E4M3), scales=x_scales[:],
                                   in_=x_grouped[k][:].rearrange("p n t -> p (n t)"))
             x_ops[k] = (x_codes, x_scales)
@@ -205,25 +199,14 @@ def tile_attend_glch_x_ts_kernel(tc, xT, wT, y, wt, ts, offs, out):
                 nc.tensor.matmul_mx(out=unread[:], lhsT=x_codes[:].bitcast(E4M3), lhsT_scale=x_scales[:],
                                     rhs=wd_codes[:].bitcast(E4M3), rhs_scale=wd_scales[:], start=True, stop=True)
 
-        def deal_targets(k):
-            y_dealt[k] = dealt.tile([P, PACK, P], F32, name="y_dealt%d" % k, align_bytes=64, offset=(k % 2) * 4 * N)
-            nc.vector.tensor_copy(y_dealt[k][:].rearrange("r (u e) (m i) -> r m u i e", e=PAIR, i=4),
-                                  y_sb[k // PAIR][:, k % PAIR, :].rearrange("r (m i u e) -> r m u i e", i=4, u=PAIR, e=PAIR))
-
         def scale_scores(k):
-            if k == 0:
-                neg_a[k] = dealt.tile([P, N], F32, name="neg_a_first", align_bytes=64, offset=0)
-            else:
-                neg_a[k] = ring.tile([P, N], F32, name="neg_a", bufs=2)
+            neg_a[k] = ring.tile([P, N], F32, name="neg_a", bufs=3)
             nc.vector.tensor_tensor(neg_a[k][:].rearrange("r (t p) -> r t p", t=PACK), sums[k][:].rearrange("r (p t) -> r t p", t=PACK), neg_ts[:], MULT)
 
         def residual(k):
             scored = [neg_a[k][:, t * P : (t + 1) * P] for t in range(PACK)]
-            if k in STEPPED:
-                wanted = [y_sb[k // PAIR][:, k % PAIR, t::PACK] for t in range(PACK)]
-            else:
-                wanted = [y_dealt[k][:, t, :] for t in range(PACK)]
-            terms = wanted + scored if k == CHUNKS - 1 else scored + wanted
+            wanted = [y_sb[k // PAIR][:, k % PAIR, t::PACK] for t in range(PACK)]
+            terms = wanted + scored
             targets[k] = psum.tile([P, PACK, P], F32, name="z%d" % k, offset=(2 + k % 2) * BANK)
             for n, term in enumerate(terms):
                 nc.tensor.matmul(targets[k][:, n % PACK, :], term, ident[:], start=(n == 0),
@@ -277,6 +260,9 @@ def tile_attend_glch_x_ts_kernel(tc, xT, wT, y, wt, ts, offs, out):
         scores(0)
         scores(1)
         turn_plane(PACK - 1)
+        load_y(2, 4 * SLOT)
+        load_x(3, 2 * SLOT + HALF)
+        load_y(3, HALF)
         interleave_x(2)
         for s in range(CHUNKS + LAG):
             each(scale_scores, s)
@@ -284,8 +270,6 @@ def tile_attend_glch_x_ts_kernel(tc, xT, wT, y, wt, ts, offs, out):
             each(quantize_x, s + 2)
             each(scores, s + 2)
             each(weigh, s - LAG)
-            if s + 1 not in STEPPED:
-                each(deal_targets, s + 1)
             if s == 0:
                 quantize_planes(1)
             each(quantize_h, s - LAG)

@@ -23,12 +23,13 @@ PACK = 4
 PAIR = 2
 QUAD = 4
 CHUNKS = R // P
-LAG = 3
+LAG = 2
+EARLY = 2
 HALF = 2 * T
 BANK = 2048
 SLOT = 4 * T
-WARM_SCORES = (2, 4)
-WARM_GRADIENT = (3, 4)
+WARM_SCORES = (1, 2)
+WARM_GRADIENT = (4, 5)
 
 
 def tile_attend_glch_x_ts_kernel(tc, xT, wT, y, wt, ts, offs, out):
@@ -168,6 +169,7 @@ def tile_attend_glch_x_ts_kernel(tc, xT, wT, y, wt, ts, offs, out):
         x_ops = {}
         sums = {}
         targets = {}
+        y_dealt = {}
         neg_a = {}
         tanhs = {}
         h = {}
@@ -199,14 +201,21 @@ def tile_attend_glch_x_ts_kernel(tc, xT, wT, y, wt, ts, offs, out):
                 nc.tensor.matmul_mx(out=unread[:], lhsT=x_codes[:].bitcast(E4M3), lhsT_scale=x_scales[:],
                                     rhs=wd_codes[:].bitcast(E4M3), rhs_scale=wd_scales[:], start=True, stop=True)
 
+        def deal_targets(k):
+            y_dealt[k] = ring.tile([P, PACK, P], F32, name="y_dealt", align_bytes=64, bufs=2)
+            nc.vector.tensor_copy(y_dealt[k][:].rearrange("r (u e) (m i) -> r m u i e", e=PAIR, i=4),
+                                  y_sb[k // PAIR][:, k % PAIR, :].rearrange("r (m i u e) -> r m u i e", i=4, u=PAIR, e=PAIR))
+
         def scale_scores(k):
             neg_a[k] = ring.tile([P, N], F32, name="neg_a", bufs=3)
             nc.vector.tensor_tensor(neg_a[k][:].rearrange("r (t p) -> r t p", t=PACK), sums[k][:].rearrange("r (p t) -> r t p", t=PACK), neg_ts[:], MULT)
 
         def residual(k):
             scored = [neg_a[k][:, t * P : (t + 1) * P] for t in range(PACK)]
-            wanted = [y_sb[k // PAIR][:, k % PAIR, t::PACK] for t in range(PACK)]
-            terms = wanted + scored
+            if k < EARLY:
+                terms = [y_sb[k // PAIR][:, k % PAIR, t::PACK] for t in range(PACK)] + scored
+            else:
+                terms = scored + [y_dealt[k][:, t, :] for t in range(PACK)]
             targets[k] = psum.tile([P, PACK, P], F32, name="z%d" % k, offset=(2 + k % 2) * BANK)
             for n, term in enumerate(terms):
                 nc.tensor.matmul(targets[k][:, n % PACK, :], term, ident[:], start=(n == 0),
@@ -270,6 +279,8 @@ def tile_attend_glch_x_ts_kernel(tc, xT, wT, y, wt, ts, offs, out):
             each(quantize_x, s + 2)
             each(scores, s + 2)
             each(weigh, s - LAG)
+            if s + 1 >= EARLY:
+                each(deal_targets, s + 1)
             if s == 0:
                 quantize_planes(1)
             each(quantize_h, s - LAG)

@@ -23,13 +23,14 @@ PACK = 4
 PAIR = 2
 QUAD = 4
 CHUNKS = R // P
-LAG = 2
+LAG = 3
 EARLY = 2
+STEPPED = (3, 5)
 HALF = 2 * T
 BANK = 2048
 SLOT = 4 * T
-WARM_SCORES = (1, 2)
-WARM_GRADIENT = (4, 5)
+WARM_SCORES = {1: 1, 3: 1}
+WARM_GRADIENT = {3: 1, 4: 1}
 
 
 def tile_attend_glch_x_ts_kernel(tc, xT, wT, y, wt, ts, offs, out):
@@ -89,7 +90,7 @@ def tile_attend_glch_x_ts_kernel(tc, xT, wT, y, wt, ts, offs, out):
             nc.tensor.transpose(ts_turned[:, t, :], ts_listed[:, t::PACK], ident[:])
         ts_part = keep.tile([P, PACK], F32, name="ts_part")
         nc.scalar.copy(ts_part[:], ts_turned[:, :, 0])
-        ts_spread = psum.tile([P, PACK, P], F32, name="ts_spread", offset=6 * BANK)
+        ts_spread = psum.tile([P, PACK, P], F32, name="ts_spread", offset=0)
         for t in range(PACK):
             nc.tensor.transpose(ts_spread[:, t, :], ts_part[:, t : t + 1].to_broadcast([P, P]), ident[:])
         neg_ts = keep.tile([P, PACK, P], F32, name="neg_ts")
@@ -144,20 +145,18 @@ def tile_attend_glch_x_ts_kernel(tc, xT, wT, y, wt, ts, offs, out):
 
         gather_plane(0)
         turn_plane(0)
-        nc.scalar.activation(neg_ts[:], ts_spread[:], ACT.Copy, scale=-1.0)
-        factor_on_scalar(0)
-        factor_on_scalar(1)
         gather_plane(1)
         load_y(0, SLOT)
         load_x(0, SLOT + HALF)
         turn_plane(1)
-        factor_on_scalar(2)
-        factor_on_scalar(3)
+        nc.scalar.activation(neg_ts[:], ts_spread[:], ACT.Copy, scale=-1.0)
         gather_plane(2)
         load_x(1, 2 * SLOT)
         quantize_planes(0)
         load_y(1, 0)
         turn_plane(2)
+        for t in range(PACK):
+            factor_on_scalar(t)
         gather_plane(3)
         load_x(2, 3 * SLOT)
         interleave_planes()
@@ -197,7 +196,7 @@ def tile_attend_glch_x_ts_kernel(tc, xT, wT, y, wt, ts, offs, out):
             sums[k] = psum.tile([P, N], F32, name="a%d" % k, offset=(k % 2) * BANK)
             nc.tensor.matmul_mx(out=sums[k][:], lhsT=x_codes[:].bitcast(E4M3), lhsT_scale=x_scales[:],
                                 rhs=wd_codes[:].bitcast(E4M3), rhs_scale=wd_scales[:], start=True, stop=True)
-            if k in WARM_SCORES:
+            for repeat in range(WARM_SCORES.get(k, 0)):
                 nc.tensor.matmul_mx(out=unread[:], lhsT=x_codes[:].bitcast(E4M3), lhsT_scale=x_scales[:],
                                     rhs=wd_codes[:].bitcast(E4M3), rhs_scale=wd_scales[:], start=True, stop=True)
 
@@ -215,28 +214,40 @@ def tile_attend_glch_x_ts_kernel(tc, xT, wT, y, wt, ts, offs, out):
             if k < EARLY:
                 terms = [y_sb[k // PAIR][:, k % PAIR, t::PACK] for t in range(PACK)] + scored
             else:
-                terms = scored + [y_dealt[k][:, t, :] for t in range(PACK)]
+                if k in STEPPED:
+                    wanted = [y_sb[k // PAIR][:, k % PAIR, t::PACK] for t in range(PACK)]
+                else:
+                    wanted = [y_dealt[k][:, t, :] for t in range(PACK)]
+                terms = wanted + scored if k == CHUNKS - 1 else scored + wanted
             targets[k] = psum.tile([P, PACK, P], F32, name="z%d" % k, offset=(2 + k % 2) * BANK)
             for n, term in enumerate(terms):
                 nc.tensor.matmul(targets[k][:, n % PACK, :], term, ident[:], start=(n == 0),
                                  stop=(n == len(terms) - 1), is_transpose=True)
 
+        def parts(k):
+            if k == CHUNKS - 1:
+                return [slice(0, P // 2), slice(P // 2, P)]
+            return [slice(0, P)]
+
         def squash(k):
             tanhs[k] = ring.tile([P, PACK, P], F32, name="tanh", bufs=LAG + 1)
-            nc.scalar.activation(tanhs[k][:], targets[k][:], ACT.Tanh, scale=-1.0)
+            for part in parts(k):
+                nc.scalar.activation(tanhs[k][:, :, part], targets[k][:, :, part], ACT.Tanh, scale=-1.0)
 
         def weigh(k):
             h[k] = ring.tile([P, P, PACK], BF16, name="h", align_bytes=64, bufs=2)
-            rows = slice((k % QUAD) * P, (k % QUAD + 1) * P)
-            nc.vector.tensor_tensor(h[k][:].rearrange("p (m i) t -> p m t i", i=PAIR),
-                                    tanhs[k][:].rearrange("p t (m i) -> p m t i", i=PAIR),
-                                    factor[k // QUAD][:, :, rows].rearrange("p t (m i) -> p m t i", i=PAIR), MULT)
+            weights = factor[k // QUAD][:, :, (k % QUAD) * P : (k % QUAD + 1) * P]
+            for part in parts(k):
+                nc.vector.tensor_tensor(h[k][:, part, :].rearrange("p (m i) t -> p m t i", i=PAIR),
+                                        tanhs[k][:, :, part].rearrange("p t (m i) -> p m t i", i=PAIR),
+                                        weights[:, :, part].rearrange("p t (m i) -> p m t i", i=PAIR), MULT)
 
         def quantize_h(k):
             h_codes = ring.tile([P, P], U32, name="h_codes", align_bytes=64, bufs=2)
             h_scales = ring.tile([P, P], U8, name="h_scales", align_bytes=64, bufs=2)
-            nc.vector.quantize_mx(out=h_codes[:].bitcast(E5M2), scales=h_scales[:],
-                                  in_=h[k][:].rearrange("p n t -> p (n t)"))
+            for part in parts(k):
+                nc.vector.quantize_mx(out=h_codes[:, part].bitcast(E5M2), scales=h_scales[:, part],
+                                      in_=h[k][:, part, :].rearrange("p n t -> p (n t)"))
             h_ops[k] = (h_codes, h_scales)
 
         def gradient(k):
@@ -244,7 +255,7 @@ def tile_attend_glch_x_ts_kernel(tc, xT, wT, y, wt, ts, offs, out):
             grads[k] = psum.tile([P, D], F32, name="grad%d" % k, offset=(5 + (k + 1) % 3) * BANK)
             nc.tensor.matmul_mx(out=grads[k][:], lhsT=h_codes[:].bitcast(E5M2), lhsT_scale=h_scales[:],
                                 rhs=wi_codes[:].bitcast(E4M3), rhs_scale=wi_scales[:], start=True, stop=True)
-            if k in WARM_GRADIENT:
+            for repeat in range(WARM_GRADIENT.get(k, 0)):
                 nc.tensor.matmul_mx(out=unread[:], lhsT=h_codes[:].bitcast(E5M2), lhsT_scale=h_scales[:],
                                     rhs=wi_codes[:].bitcast(E4M3), rhs_scale=wi_scales[:], start=True, stop=True)
 
@@ -252,11 +263,13 @@ def tile_attend_glch_x_ts_kernel(tc, xT, wT, y, wt, ts, offs, out):
             result = ring.tile([P, D], F32, name="result", bufs=CHUNKS)
             natural = result[:].rearrange("r (p t) -> r p t", t=PACK)
             planes = grads[k][:].rearrange("r (t p) -> r p t", t=PACK)
-            if k == CHUNKS - 1:
-                nc.vector.tensor_copy(natural, planes)
-            else:
-                nc.scalar.copy(natural, planes)
-            nc.sync.dma_start(out_rows[k], result[:])
+            for part in parts(k):
+                if k == CHUNKS - 1:
+                    nc.vector.tensor_copy(natural[:, part], planes[:, part])
+                else:
+                    nc.scalar.copy(natural[:, part], planes[:, part])
+                cols = slice(part.start * PACK, part.stop * PACK)
+                nc.sync.dma_start(out_rows[k][:, cols], result[:, cols])
 
         def each(stage, k):
             if 0 <= k < CHUNKS:
@@ -279,7 +292,7 @@ def tile_attend_glch_x_ts_kernel(tc, xT, wT, y, wt, ts, offs, out):
             each(quantize_x, s + 2)
             each(scores, s + 2)
             each(weigh, s - LAG)
-            if s + 1 >= EARLY:
+            if s + 1 >= EARLY and s + 1 not in STEPPED:
                 each(deal_targets, s + 1)
             if s == 0:
                 quantize_planes(1)

@@ -30,7 +30,7 @@ HALF = 2 * T
 BANK = 2048
 SLOT = 4 * T
 WARM_SCORES = {1: 1, 3: 1}
-WARM_GRADIENT = {3: 1, 4: 1}
+WARM_GRADIENT = {3: 1}
 
 
 def tile_attend_glch_x_ts_kernel(tc, xT, wT, y, wt, ts, offs, out):
@@ -69,8 +69,6 @@ def tile_attend_glch_x_ts_kernel(tc, xT, wT, y, wt, ts, offs, out):
 
         ident = keep.tile([P, P], F32, name="ident")
         make_identity(nc, ident[:])
-        warm = keep.tile([P, 1], F32, name="warm")
-        nc.scalar.activation(warm[:], ident[:, 0:1], ACT.Tanh)
 
         ts_listed = keep.tile([P, N], F32, name="ts_listed")
         nc.vector.tensor_copy(ts_listed[:], ts_window[:].indirect(offsets[:]))
@@ -102,13 +100,13 @@ def tile_attend_glch_x_ts_kernel(tc, xT, wT, y, wt, ts, offs, out):
         for t in range(PACK):
             nc.gpsimd.tensor_scalar(factor[1][:, t, :], wt_row[:, R // 2 : R], ts_part[:, t : t + 1], 0.0, MULT, ADD)
 
-        w_listed = stage.tile([P, N, PACK], BF16, name="w_listed", align_bytes=64, offset=2 * SLOT + HALF)
+        w_listed = stage.tile([P, N, PACK], BF16, name="w_listed", align_bytes=64, offset=5 * SLOT + HALF // 2)
         wd_codes = keep.tile([P, N], U32, name="wd_codes", align_bytes=64)
         wd_scales = keep.tile([P, N], U8, name="wd_scales", align_bytes=64)
         wi_codes = keep.tile([P, D], U32, name="wi_codes", align_bytes=64)
         wi_scales = keep.tile([P, D], U8, name="wi_scales", align_bytes=64)
         w_turned = [stage.tile([P, PAIR, P, PACK], BF16, name="w_turned0", align_bytes=64, offset=0),
-                    keep.tile([P, PAIR, P, PACK], BF16, name="w_turned1", align_bytes=64)]
+                    stage.tile([P, PAIR, P, PACK], BF16, name="w_turned1", align_bytes=64, offset=HALF)]
 
         planes = stage.tile([P, PACK * N], BF16, name="planes", align_bytes=64, offset=4 * SLOT)
 
@@ -154,7 +152,6 @@ def tile_attend_glch_x_ts_kernel(tc, xT, wT, y, wt, ts, offs, out):
         load_x(1, 2 * SLOT)
         quantize_planes(0)
         load_y(1, 0)
-        turn_plane(2)
         for t in range(PACK):
             factor_on_scalar(t)
         gather_plane(3)
@@ -182,11 +179,11 @@ def tile_attend_glch_x_ts_kernel(tc, xT, wT, y, wt, ts, offs, out):
             nc.scalar.copy(dst, src)
 
         def quantize_x(k):
+            x_codes = stage.tile([P, P], U32, name="x_codes%d" % k, align_bytes=64, offset=6 * SLOT + (k % 2) * 4 * P)
             if k == 0:
-                x_codes = stage.tile([P, P], U32, name="x_codes_first", align_bytes=64, offset=HALF)
+                x_scales = stage.tile([P, P], U8, name="x_scales_first", align_bytes=64, offset=HALF)
             else:
-                x_codes = ring.tile([P, P], U32, name="x_codes", align_bytes=64, bufs=2)
-            x_scales = ring.tile([P, P], U8, name="x_scales", align_bytes=64, bufs=3)
+                x_scales = ring.tile([P, P], U8, name="x_scales", align_bytes=64, bufs=2)
             nc.vector.quantize_mx(out=x_codes[:].bitcast(E4M3), scales=x_scales[:],
                                   in_=x_grouped[k][:].rearrange("p n t -> p (n t)"))
             x_ops[k] = (x_codes, x_scales)
@@ -281,23 +278,27 @@ def tile_attend_glch_x_ts_kernel(tc, xT, wT, y, wt, ts, offs, out):
         quantize_x(1)
         scores(0)
         scores(1)
+        turn_plane(2)
         turn_plane(PACK - 1)
         load_y(2, 4 * SLOT)
-        load_x(3, 2 * SLOT + HALF)
-        load_y(3, HALF)
+        load_x(3, 5 * SLOT)
+        load_y(3, 5 * SLOT + HALF)
         interleave_x(2)
-        for s in range(CHUNKS + LAG):
+        for s in range(CHUNKS + LAG + 1):
             each(scale_scores, s)
             each(residual, s)
+            each(weigh, s - LAG)
             each(quantize_x, s + 2)
             each(scores, s + 2)
-            each(weigh, s - LAG)
             if s + 1 >= EARLY and s + 1 not in STEPPED:
                 each(deal_targets, s + 1)
             if s == 0:
                 quantize_planes(1)
-            each(quantize_h, s - LAG)
-            each(gradient, s - LAG)
+            done = s - LAG if s < CHUNKS - 1 else s - LAG - 1
+            if s != CHUNKS - 1:
+                each(quantize_h, done)
+                each(gradient, done)
             each(squash, s)
             each(interleave_x, s + 3)
-            each(store, s - LAG)
+            if s != CHUNKS - 1:
+                each(store, done)

@@ -16,7 +16,6 @@ E4M3 = mybir.dt.float8_e4m3fn_x4
 E5M2 = mybir.dt.float8_e5m2_x4
 ACT = mybir.ActivationFunctionType
 MULT = mybir.AluOpType.mult
-ADD = mybir.AluOpType.add
 
 P = 128
 PACK = 4
@@ -24,6 +23,7 @@ PAIR = 2
 QUAD = 4
 CHUNKS = R // P
 LAG = 3
+SCALAR_SLOTS = 128
 EARLY = 2
 STEPPED = (3, 5)
 HALF = 2 * T
@@ -46,89 +46,101 @@ def tile_attend_glch_x_ts_kernel(tc, xT, wT, y, wt, ts, offs, out):
         y_rows = y[0].rearrange("(c j p) i -> c p j i", p=P, j=PAIR)
         out_rows = out[0].rearrange("(k p) d -> k p d", p=P)
 
-        ts_row = stage.tile([1, T], F32, name="ts_row", align_bytes=64, offset=4 * SLOT)
+        ts_row = stage.tile([1, T], F32, name="ts_row", align_bytes=64, offset=7 * SLOT)
         nc.sync.dma_start(ts_row[:], ts[0:1, :])
         wt_sb = keep.tile([P, R // P], F32, name="wt_sb")
         nc.sync.dma_start(wt_sb[:], wt[0].rearrange("(p k) o -> p (k o)", p=P))
         offsets = keep.tile([P, N // 16], U16, name="offsets")
         nc.sync.dma_start(offsets[:], offs)
 
-        ts_window = stage.tile([P, T], F32, name="ts_window", align_bytes=64, offset=(PACK - 1) * SLOT)
+        ts_window = stage.tile([P, T], F32, name="ts_window", align_bytes=64, offset=4 * SLOT)
         w_plane = {}
 
         def load_plane(t):
             w_plane[t] = stage.tile([P, T], F32, name="w_plane%d" % t, align_bytes=64, offset=t * SLOT)
             nc.sync.dma_start(w_plane[t][:], w_rows[t])
 
-        for t in range(PACK - 1):
+        for t in range(PACK):
             load_plane(t)
 
-        nc.vector.memset(ts_window[:, 0 : T // 2], 0.0)
-        nc.gpsimd.memset(ts_window[:, T // 2 : T], 0.0)
+        nc.vector.memset(ts_window[:], 0.0)
         nc.vector.tensor_copy(ts_window[0:1, :], ts_row[:])
 
         ident = keep.tile([P, P], F32, name="ident")
         make_identity(nc, ident[:])
 
-        ts_listed = keep.tile([P, N], F32, name="ts_listed")
+        ts_listed = stage.tile([P, N], F32, name="ts_listed", align_bytes=64, offset=10 * SLOT)
         nc.vector.tensor_copy(ts_listed[:], ts_window[:].indirect(offsets[:]))
-        load_plane(PACK - 1)
 
-        wt_row = keep.tile([P, R], F32, name="wt_row")
+        first_rows = stage.tile([P, PAIR, HALF // 4], F32, name="first_rows", align_bytes=64, offset=8 * SLOT)
+        last_rows = keep.tile([P, PAIR, PAIR * P], F32, name="last_rows")
+        wt_row = [first_rows[:, :, 0 : PAIR * P], last_rows[:]]
+        wt_spreads = []
         for half in range(2):
             wt_spread = psum.tile([P, 4, P], F32, name="wt_spread%d" % half, offset=(2 + half) * BANK)
             for k in range(4):
                 col = 4 * half + k
                 nc.tensor.transpose(wt_spread[:, k, :], wt_sb[:, col : col + 1].to_broadcast([P, P]), ident[:])
-            nc.scalar.copy(wt_row[:].rearrange("p (n k) -> p n k", k=8)[:, :, 4 * half : 4 * half + 4],
-                           wt_spread[:].rearrange("p k n -> p n k"))
+            wt_spreads.append(wt_spread)
+        for rows in range(2):
+            for half in range(2):
+                nc.scalar.copy(wt_row[rows].rearrange("p c (n k) -> p c n k", k=8)[:, :, :, 4 * half : 4 * half + 4],
+                               wt_spreads[half][:, :, rows * (P // 2) : (rows + 1) * (P // 2)].rearrange("p k (c n) -> p c n k", c=PAIR))
 
         ts_turned = psum.tile([P, PACK, P], F32, name="ts_turned", offset=5 * BANK)
         for t in range(PACK):
             nc.tensor.transpose(ts_turned[:, t, :], ts_listed[:, t::PACK], ident[:])
         ts_part = keep.tile([P, PACK], F32, name="ts_part")
         nc.scalar.copy(ts_part[:], ts_turned[:, :, 0])
-        ts_spread = psum.tile([P, PACK, P], F32, name="ts_spread", offset=0)
+        ts_spread = psum.tile([P, PACK, P], F32, name="ts_spread", offset=7 * BANK)
         for t in range(PACK):
             nc.tensor.transpose(ts_spread[:, t, :], ts_part[:, t : t + 1].to_broadcast([P, P]), ident[:])
         neg_ts = keep.tile([P, PACK, P], F32, name="neg_ts")
         factor = [keep.tile([P, PACK, R // 2], F32, name="factor%d" % half) for half in range(2)]
 
-        def factor_on_scalar(t):
-            nc.scalar.activation(factor[0][:, t, :], wt_row[:, 0 : R // 2], ACT.Copy, scale=ts_part[:, t : t + 1])
+        def factor_on_scalar(half, t):
+            nc.scalar.activation(factor[half][:, t, :].rearrange("p (c n) -> p c n", c=PAIR), wt_row[half], ACT.Copy, scale=ts_part[:, t : t + 1])
 
-        for t in range(PACK):
-            nc.gpsimd.tensor_scalar(factor[1][:, t, :], wt_row[:, R // 2 : R], ts_part[:, t : t + 1], 0.0, MULT, ADD)
+        def factor_on_vector(half, t):
+            nc.vector.tensor_scalar(factor[half][:, t, :].rearrange("p (c n) -> p c n", c=PAIR), wt_row[half], ts_part[:, t : t + 1], None, MULT)
 
         w_listed = stage.tile([P, N, PACK], BF16, name="w_listed", align_bytes=64, offset=5 * SLOT + HALF // 2)
         wd_codes = keep.tile([P, N], U32, name="wd_codes", align_bytes=64)
         wd_scales = keep.tile([P, N], U8, name="wd_scales", align_bytes=64)
         wi_codes = keep.tile([P, D], U32, name="wi_codes", align_bytes=64)
         wi_scales = keep.tile([P, D], U8, name="wi_scales", align_bytes=64)
-        w_turned = [stage.tile([P, PAIR, P, PACK], BF16, name="w_turned0", align_bytes=64, offset=0),
-                    stage.tile([P, PAIR, P, PACK], BF16, name="w_turned1", align_bytes=64, offset=HALF)]
+        planes = stage.tile([P, (PACK + 1) * N], BF16, name="planes", align_bytes=64, offset=4 * SLOT)
+        late_turned = stage.tile([P, PAIR * N], BF16, name="late_turned", align_bytes=64, offset=HALF)
+        w_turned = [planes[:, (PACK - 1) * N : (PACK + 1) * N], late_turned[:]]
 
-        planes = stage.tile([P, PACK * N], BF16, name="planes", align_bytes=64, offset=4 * SLOT)
-
-        def gather_plane(t):
-            nc.vector.tensor_copy(planes[:, t * N : (t + 1) * N], w_plane[t][:].indirect(offsets[:]))
+        def gather_plane(t, pieces=1):
+            width = N // pieces
+            for j in range(pieces):
+                nc.vector.tensor_copy(planes[:, t * N + j * width : t * N + (j + 1) * width],
+                                      w_plane[t][:].indirect(offsets[:, j * width // 16 : (j + 1) * width // 16]))
 
         def turn_plane(t):
-            bank = psum.tile([P, PAIR, P], F32, name="w_bank%d" % t, offset=(5 + t % 3) * BANK)
+            bank = psum.tile([P, PAIR, P], F32, name="w_bank%d" % t, offset=(6, 5, 5, 6)[t] * BANK)
             words = planes[:, t * N : (t + 1) * N].bitcast(F32)
             for u in range(PAIR):
                 nc.tensor.transpose(bank[:, u, :], words[:, u::PAIR], ident[:])
-            nc.scalar.copy(w_turned[t // PAIR][:, t % PAIR].rearrange("q p s -> q (p s)").bitcast(F32).rearrange("q (p u) -> q p u", u=PAIR),
+            nc.scalar.copy(w_turned[t // PAIR][:, (t % PAIR) * N : (t % PAIR + 1) * N].bitcast(F32).rearrange("q (p u) -> q p u", u=PAIR),
                            bank[:].rearrange("q u p -> q p u"))
 
-        def interleave_planes():
-            nc.vector.tensor_copy(w_listed[:].rearrange("p (m i) t -> p m t i", i=4),
-                                  planes[:].rearrange("p (t m i) -> p m t i", t=PACK, i=4))
+        def interleave_planes(copy, first, last):
+            runs = slice(first // 4, last // 4)
+            copy(w_listed[:].rearrange("p (m i) t -> p m t i", i=4)[:, runs],
+                 planes[:, 0 : PACK * N].rearrange("p (t m i) -> p m t i", t=PACK, i=4)[:, runs])
+
+        def quantize_listed(half):
+            cols = slice(half * N // 2, (half + 1) * N // 2)
+            nc.vector.quantize_mx(out=wd_codes[:, cols].bitcast(E4M3), scales=wd_scales[:, cols],
+                                  in_=w_listed[:, cols, :].rearrange("p i t -> p (i t)"))
 
         def quantize_planes(u):
             cols = slice(u * PAIR * P, (u + 1) * PAIR * P)
             nc.vector.quantize_mx(out=wi_codes[:, cols].bitcast(E4M3), scales=wi_scales[:, cols],
-                                  in_=w_turned[u][:].rearrange("q t p s -> q (t p s)"))
+                                  in_=w_turned[u])
 
         x_raw = {}
         y_sb = {}
@@ -141,24 +153,29 @@ def tile_attend_glch_x_ts_kernel(tc, xT, wT, y, wt, ts, offs, out):
             y_sb[pair] = stage.tile([P, PAIR, N], F32, name="y_sb%d" % pair, align_bytes=64, offset=offset)
             nc.sync.dma_start(y_sb[pair][:], y_rows[pair])
 
+        load_y(0, 10 * SLOT)
         gather_plane(0)
         turn_plane(0)
         gather_plane(1)
-        load_y(0, SLOT)
-        load_x(0, SLOT + HALF)
+        for t in range(PACK):
+            factor_on_scalar(0, t)
+        load_x(0, 8 * SLOT)
+        load_x(1, 8 * SLOT + HALF)
         turn_plane(1)
         nc.scalar.activation(neg_ts[:], ts_spread[:], ACT.Copy, scale=-1.0)
         gather_plane(2)
-        load_x(1, 2 * SLOT)
+        for t in range(PAIR):
+            factor_on_scalar(1, t)
+            factor_on_vector(1, PAIR + t)
         quantize_planes(0)
-        load_y(1, 0)
-        for t in range(PACK):
-            factor_on_scalar(t)
-        gather_plane(3)
-        load_x(2, 3 * SLOT)
-        interleave_planes()
-        nc.vector.quantize_mx(out=wd_codes[:].bitcast(E4M3), scales=wd_scales[:],
-                              in_=w_listed[:].rearrange("p i t -> p (i t)"))
+        gather_plane(3, PAIR)
+        load_y(1, 3 * SLOT)
+        load_x(2, 3 * SLOT + HALF)
+        interleave_planes(nc.scalar.copy, 0, SCALAR_SLOTS)
+        interleave_planes(nc.vector.tensor_copy, SCALAR_SLOTS, N // 2)
+        interleave_planes(nc.vector.tensor_copy, N // 2, N)
+        quantize_listed(0)
+        quantize_listed(1)
 
         unread = psum.tile([P, N], F32, name="unread", offset=4 * BANK)
         x_grouped = {}

@@ -29,6 +29,7 @@ STEPPED = (3, 5)
 HALF = 2 * T
 BANK = 2048
 SLOT = 4 * T
+WARM = 256
 WARM_SCORES = {1: 1, 3: 1}
 WARM_GRADIENT = {3: 1}
 
@@ -177,7 +178,7 @@ def tile_attend_glch_x_ts_kernel(tc, xT, wT, y, wt, ts, offs, out):
         quantize_listed(0)
         quantize_listed(1)
 
-        unread = psum.tile([P, N], F32, name="unread", offset=4 * BANK)
+        unread = psum.tile([P, WARM], F32, name="unread", offset=4 * BANK)
         x_grouped = {}
         x_ops = {}
         sums = {}
@@ -212,7 +213,7 @@ def tile_attend_glch_x_ts_kernel(tc, xT, wT, y, wt, ts, offs, out):
                                 rhs=wd_codes[:].bitcast(E4M3), rhs_scale=wd_scales[:], start=True, stop=True)
             for repeat in range(WARM_SCORES.get(k, 0)):
                 nc.tensor.matmul_mx(out=unread[:], lhsT=x_codes[:].bitcast(E4M3), lhsT_scale=x_scales[:],
-                                    rhs=wd_codes[:].bitcast(E4M3), rhs_scale=wd_scales[:], start=True, stop=True)
+                                    rhs=wd_codes[:, 0:WARM].bitcast(E4M3), rhs_scale=wd_scales[:, 0:WARM], start=True, stop=True)
 
         def deal_targets(k):
             y_dealt[k] = ring.tile([P, PACK, P], F32, name="y_dealt", align_bytes=64, bufs=2)
@@ -271,7 +272,7 @@ def tile_attend_glch_x_ts_kernel(tc, xT, wT, y, wt, ts, offs, out):
                                 rhs=wi_codes[:].bitcast(E4M3), rhs_scale=wi_scales[:], start=True, stop=True)
             for repeat in range(WARM_GRADIENT.get(k, 0)):
                 nc.tensor.matmul_mx(out=unread[:], lhsT=h_codes[:].bitcast(E5M2), lhsT_scale=h_scales[:],
-                                    rhs=wi_codes[:].bitcast(E4M3), rhs_scale=wi_scales[:], start=True, stop=True)
+                                    rhs=wi_codes[:, 0:WARM].bitcast(E4M3), rhs_scale=wi_scales[:, 0:WARM], start=True, stop=True)
 
         def store(k):
             result = ring.tile([P, D], F32, name="result", bufs=CHUNKS)

from contextlib import ExitStack

import concourse.mybir as mybir
from concourse.masks import make_identity

N, T, D, R = 512, 2048, 512, 1024
FLOPS = 2 * 2 * R * N * D
BYTES = 4 * (D * R + D * T + R * N + R + T + R * D) + 2 * 128 * (N // 16)

F32 = mybir.dt.float32
BF16 = mybir.dt.bfloat16
U32 = mybir.dt.uint32
U16 = mybir.dt.uint16
U8 = mybir.dt.uint8
E4M3 = mybir.dt.float8_e4m3fn_x4
E5M2 = mybir.dt.float8_e5m2_x4
ACT = mybir.ActivationFunctionType
MULT = mybir.AluOpType.mult

P = 128
PACK = 4
PAIR = 2
QUAD = 4
CHUNKS = R // P
LAG = 3
SCALAR_SLOTS = 128
EARLY = 2
STEPPED = (3, 5)
HALF = 2 * T
BANK = 2048
SLOT = 4 * T
WARM = 256
WARM_SCORES = {1: 1, 3: 1}
WARM_GRADIENT = {3: 1}


def tile_attend_glch_x_ts_kernel(tc, xT, wT, y, wt, ts, offs, out):
    nc = tc.nc
    with ExitStack() as ctx:
        keep = ctx.enter_context(tc.tile_pool(name="keep", bufs=1))
        ring = ctx.enter_context(tc.tile_pool(name="ring", bufs=4))
        stage = ctx.enter_context(tc.tile_pool(name="stage", bufs=1))
        psum = ctx.enter_context(tc.psum_pool(name="psum", bufs=1))

        w_rows = wT.rearrange("(p t) c -> t p c", t=PACK)
        x_rows = xT[0].rearrange("(p t) r -> p t r", t=PACK)
        y_rows = y[0].rearrange("(c j p) i -> c p j i", p=P, j=PAIR)
        out_rows = out[0].rearrange("(k p) d -> k p d", p=P)

        ts_row = stage.tile([1, T], F32, name="ts_row", align_bytes=64, offset=7 * SLOT)
        nc.sync.dma_start(ts_row[:], ts[0:1, :])
        wt_sb = keep.tile([P, R // P], F32, name="wt_sb")
        nc.sync.dma_start(wt_sb[:], wt[0].rearrange("(p k) o -> p (k o)", p=P))
        offsets = keep.tile([P, N // 16], U16, name="offsets")
        nc.sync.dma_start(offsets[:], offs)

        ts_window = stage.tile([P, T], F32, name="ts_window", align_bytes=64, offset=4 * SLOT)
        w_plane = {}

        def load_plane(t):
            w_plane[t] = stage.tile([P, T], F32, name="w_plane%d" % t, align_bytes=64, offset=t * SLOT)
            nc.sync.dma_start(w_plane[t][:], w_rows[t])

        for t in range(PACK):
            load_plane(t)

        nc.vector.memset(ts_window[:], 0.0)
        nc.vector.tensor_copy(ts_window[0:1, :], ts_row[:])

        ident = keep.tile([P, P], F32, name="ident")
        make_identity(nc, ident[:])

        ts_listed = stage.tile([P, N], F32, name="ts_listed", align_bytes=64, offset=10 * SLOT)
        nc.vector.tensor_copy(ts_listed[:], ts_window[:].indirect(offsets[:]))

        first_rows = stage.tile([P, PAIR, HALF // 4], F32, name="first_rows", align_bytes=64, offset=8 * SLOT)
        last_rows = keep.tile([P, PAIR, PAIR * P], F32, name="last_rows")
        wt_row = [first_rows[:, :, 0 : PAIR * P], last_rows[:]]
        wt_spreads = []
        for half in range(2):
            wt_spread = psum.tile([P, 4, P], F32, name="wt_spread%d" % half, offset=(2 + half) * BANK)
            for k in range(4):
                col = 4 * half + k
                nc.tensor.transpose(wt_spread[:, k, :], wt_sb[:, col : col + 1].to_broadcast([P, P]), ident[:])
            wt_spreads.append(wt_spread)
        for rows in range(2):
            for half in range(2):
                nc.scalar.copy(wt_row[rows].rearrange("p c (n k) -> p c n k", k=8)[:, :, :, 4 * half : 4 * half + 4],
                               wt_spreads[half][:, :, rows * (P // 2) : (rows + 1) * (P // 2)].rearrange("p k (c n) -> p c n k", c=PAIR))

        ts_turned = psum.tile([P, PACK, P], F32, name="ts_turned", offset=5 * BANK)
        for t in range(PACK):
            nc.tensor.transpose(ts_turned[:, t, :], ts_listed[:, t::PACK], ident[:])
        ts_part = keep.tile([P, PACK], F32, name="ts_part")
        nc.scalar.copy(ts_part[:], ts_turned[:, :, 0])
        ts_spread = psum.tile([P, PACK, P], F32, name="ts_spread", offset=7 * BANK)
        for t in range(PACK):
            nc.tensor.transpose(ts_spread[:, t, :], ts_part[:, t : t + 1].to_broadcast([P, P]), ident[:])
        neg_ts = keep.tile([P, PACK, P], F32, name="neg_ts")
        factor = [keep.tile([P, PACK, R // 2], F32, name="factor%d" % half) for half in range(2)]

        def factor_on_scalar(half, t):
            nc.scalar.activation(factor[half][:, t, :].rearrange("p (c n) -> p c n", c=PAIR), wt_row[half], ACT.Copy, scale=ts_part[:, t : t + 1])

        def factor_on_vector(half, t):
            nc.vector.tensor_scalar(factor[half][:, t, :].rearrange("p (c n) -> p c n", c=PAIR), wt_row[half], ts_part[:, t : t + 1], None, MULT)

        w_listed = stage.tile([P, N, PACK], BF16, name="w_listed", align_bytes=64, offset=5 * SLOT + HALF // 2)
        wd_codes = keep.tile([P, N], U32, name="wd_codes", align_bytes=64)
        wd_scales = keep.tile([P, N], U8, name="wd_scales", align_bytes=64)
        wi_codes = keep.tile([P, D], U32, name="wi_codes", align_bytes=64)
        wi_scales = keep.tile([P, D], U8, name="wi_scales", align_bytes=64)
        planes = stage.tile([P, (PACK + 1) * N], BF16, name="planes", align_bytes=64, offset=4 * SLOT)
        late_turned = stage.tile([P, PAIR * N], BF16, name="late_turned", align_bytes=64, offset=HALF)
        w_turned = [planes[:, (PACK - 1) * N : (PACK + 1) * N], late_turned[:]]

        def gather_plane(t, pieces=1):
            width = N // pieces
            for j in range(pieces):
                nc.vector.tensor_copy(planes[:, t * N + j * width : t * N + (j + 1) * width],
                                      w_plane[t][:].indirect(offsets[:, j * width // 16 : (j + 1) * width // 16]))

        def turn_plane(t):
            bank = psum.tile([P, PAIR, P], F32, name="w_bank%d" % t, offset=(6, 5, 5, 6)[t] * BANK)
            words = planes[:, t * N : (t + 1) * N].bitcast(F32)
            for u in range(PAIR):
                nc.tensor.transpose(bank[:, u, :], words[:, u::PAIR], ident[:])
            nc.scalar.copy(w_turned[t // PAIR][:, (t % PAIR) * N : (t % PAIR + 1) * N].bitcast(F32).rearrange("q (p u) -> q p u", u=PAIR),
                           bank[:].rearrange("q u p -> q p u"))

        def interleave_planes(copy, first, last):
            runs = slice(first // 4, last // 4)
            copy(w_listed[:].rearrange("p (m i) t -> p m t i", i=4)[:, runs],
                 planes[:, 0 : PACK * N].rearrange("p (t m i) -> p m t i", t=PACK, i=4)[:, runs])

        def quantize_listed(half):
            cols = slice(half * N // 2, (half + 1) * N // 2)
            nc.vector.quantize_mx(out=wd_codes[:, cols].bitcast(E4M3), scales=wd_scales[:, cols],
                                  in_=w_listed[:, cols, :].rearrange("p i t -> p (i t)"))

        def quantize_planes(u):
            cols = slice(u * PAIR * P, (u + 1) * PAIR * P)
            nc.vector.quantize_mx(out=wi_codes[:, cols].bitcast(E4M3), scales=wi_scales[:, cols],
                                  in_=w_turned[u])

        x_raw = {}
        y_sb = {}

        def load_x(pair, offset):
            x_raw[pair] = stage.tile([P, PACK, PAIR * P], F32, name="x_raw%d" % pair, align_bytes=64, offset=offset)
            nc.sync.dma_start(x_raw[pair][:], x_rows[:, :, pair * P * PAIR : (pair + 1) * P * PAIR])

        def load_y(pair, offset):
            y_sb[pair] = stage.tile([P, PAIR, N], F32, name="y_sb%d" % pair, align_bytes=64, offset=offset)
            nc.sync.dma_start(y_sb[pair][:], y_rows[pair])

        load_y(0, 10 * SLOT)
        gather_plane(0)
        turn_plane(0)
        gather_plane(1)
        for t in range(PACK):
            factor_on_scalar(0, t)
        load_x(0, 8 * SLOT)
        load_x(1, 8 * SLOT + HALF)
        turn_plane(1)
        nc.scalar.activation(neg_ts[:], ts_spread[:], ACT.Copy, scale=-1.0)
        gather_plane(2)
        for t in range(PAIR):
            factor_on_scalar(1, t)
            factor_on_vector(1, PAIR + t)
        quantize_planes(0)
        gather_plane(3, PAIR)
        load_y(1, 3 * SLOT)
        load_x(2, 3 * SLOT + HALF)
        interleave_planes(nc.scalar.copy, 0, SCALAR_SLOTS)
        interleave_planes(nc.vector.tensor_copy, SCALAR_SLOTS, N // 2)
        interleave_planes(nc.vector.tensor_copy, N // 2, N)
        quantize_listed(0)
        quantize_listed(1)

        unread = psum.tile([P, WARM], F32, name="unread", offset=4 * BANK)
        x_grouped = {}
        x_ops = {}
        sums = {}
        targets = {}
        y_dealt = {}
        neg_a = {}
        tanhs = {}
        h = {}
        h_ops = {}
        grads = {}

        def interleave_x(k):
            x_grouped[k] = ring.tile([P, P, PACK], BF16, name="x_grouped", align_bytes=64, bufs=3)
            dst = x_grouped[k][:].rearrange("p (m i) t -> p m t i", i=PAIR)
            src = x_raw[k // PAIR][:, :, (k % PAIR) * P : (k % PAIR + 1) * P].rearrange("p t (m i) -> p m t i", i=PAIR)
            nc.scalar.copy(dst, src)

        def quantize_x(k):
            x_codes = stage.tile([P, P], U32, name="x_codes%d" % k, align_bytes=64, offset=6 * SLOT + (k % 2) * 4 * P)
            if k == 0:
                x_scales = stage.tile([P, P], U8, name="x_scales_first", align_bytes=64, offset=HALF)
            else:
                x_scales = ring.tile([P, P], U8, name="x_scales", align_bytes=64, bufs=2)
            nc.vector.quantize_mx(out=x_codes[:].bitcast(E4M3), scales=x_scales[:],
                                  in_=x_grouped[k][:].rearrange("p n t -> p (n t)"))
            x_ops[k] = (x_codes, x_scales)

        def scores(k):
            x_codes, x_scales = x_ops[k]
            sums[k] = psum.tile([P, N], F32, name="a%d" % k, offset=(k % 2) * BANK)
            nc.tensor.matmul_mx(out=sums[k][:], lhsT=x_codes[:].bitcast(E4M3), lhsT_scale=x_scales[:],
                                rhs=wd_codes[:].bitcast(E4M3), rhs_scale=wd_scales[:], start=True, stop=True)
            for repeat in range(WARM_SCORES.get(k, 0)):
                nc.tensor.matmul_mx(out=unread[:], lhsT=x_codes[:].bitcast(E4M3), lhsT_scale=x_scales[:],
                                    rhs=wd_codes[:, 0:WARM].bitcast(E4M3), rhs_scale=wd_scales[:, 0:WARM], start=True, stop=True)

        def deal_targets(k):
            y_dealt[k] = ring.tile([P, PACK, P], F32, name="y_dealt", align_bytes=64, bufs=2)
            nc.vector.tensor_copy(y_dealt[k][:].rearrange("r (u e) (m i) -> r m u i e", e=PAIR, i=4),
                                  y_sb[k // PAIR][:, k % PAIR, :].rearrange("r (m i u e) -> r m u i e", i=4, u=PAIR, e=PAIR))

        def scale_scores(k):
            neg_a[k] = ring.tile([P, N], F32, name="neg_a", bufs=3)
            nc.vector.tensor_tensor(neg_a[k][:].rearrange("r (t p) -> r t p", t=PACK), sums[k][:].rearrange("r (p t) -> r t p", t=PACK), neg_ts[:], MULT)

        def residual(k):
            scored = [neg_a[k][:, t * P : (t + 1) * P] for t in range(PACK)]
            if k < EARLY:
                terms = [y_sb[k // PAIR][:, k % PAIR, t::PACK] for t in range(PACK)] + scored
            else:
                if k in STEPPED:
                    wanted = [y_sb[k // PAIR][:, k % PAIR, t::PACK] for t in range(PACK)]
                else:
                    wanted = [y_dealt[k][:, t, :] for t in range(PACK)]
                terms = wanted + scored if k == CHUNKS - 1 else scored + wanted
            targets[k] = psum.tile([P, PACK, P], F32, name="z%d" % k, offset=(2 + k % 2) * BANK)
            for n, term in enumerate(terms):
                nc.tensor.matmul(targets[k][:, n % PACK, :], term, ident[:], start=(n == 0),
                                 stop=(n == len(terms) - 1), is_transpose=True)

        def parts(k):
            if k == CHUNKS - 1:
                return [slice(0, P // 2), slice(P // 2, P)]
            return [slice(0, P)]

        def squash(k):
            tanhs[k] = ring.tile([P, PACK, P], F32, name="tanh", bufs=LAG + 1)
            for part in parts(k):
                nc.scalar.activation(tanhs[k][:, :, part], targets[k][:, :, part], ACT.Tanh, scale=-1.0)

        def weigh(k):
            h[k] = ring.tile([P, P, PACK], BF16, name="h", align_bytes=64, bufs=2)
            weights = factor[k // QUAD][:, :, (k % QUAD) * P : (k % QUAD + 1) * P]
            for part in parts(k):
                nc.vector.tensor_tensor(h[k][:, part, :].rearrange("p (m i) t -> p m t i", i=PAIR),
                                        tanhs[k][:, :, part].rearrange("p t (m i) -> p m t i", i=PAIR),
                                        weights[:, :, part].rearrange("p t (m i) -> p m t i", i=PAIR), MULT)

        def quantize_h(k):
            h_codes = ring.tile([P, P], U32, name="h_codes", align_bytes=64, bufs=2)
            h_scales = ring.tile([P, P], U8, name="h_scales", align_bytes=64, bufs=2)
            for part in parts(k):
                nc.vector.quantize_mx(out=h_codes[:, part].bitcast(E5M2), scales=h_scales[:, part],
                                      in_=h[k][:, part, :].rearrange("p n t -> p (n t)"))
            h_ops[k] = (h_codes, h_scales)

        def gradient(k):
            h_codes, h_scales = h_ops[k]
            grads[k] = psum.tile([P, D], F32, name="grad%d" % k, offset=(5 + (k + 1) % 3) * BANK)
            nc.tensor.matmul_mx(out=grads[k][:], lhsT=h_codes[:].bitcast(E5M2), lhsT_scale=h_scales[:],
                                rhs=wi_codes[:].bitcast(E4M3), rhs_scale=wi_scales[:], start=True, stop=True)
            for repeat in range(WARM_GRADIENT.get(k, 0)):
                nc.tensor.matmul_mx(out=unread[:], lhsT=h_codes[:].bitcast(E5M2), lhsT_scale=h_scales[:],
                                    rhs=wi_codes[:, 0:WARM].bitcast(E4M3), rhs_scale=wi_scales[:, 0:WARM], start=True, stop=True)

        def store(k):
            result = ring.tile([P, D], F32, name="result", bufs=CHUNKS)
            natural = result[:].rearrange("r (p t) -> r p t", t=PACK)
            planes = grads[k][:].rearrange("r (t p) -> r p t", t=PACK)
            for part in parts(k):
                if k == CHUNKS - 1:
                    nc.vector.tensor_copy(natural[:, part], planes[:, part])
                else:
                    nc.scalar.copy(natural[:, part], planes[:, part])
                cols = slice(part.start * PACK, part.stop * PACK)
                nc.sync.dma_start(out_rows[k][:, cols], result[:, cols])

        def each(stage, k):
            if 0 <= k < CHUNKS:
                stage(k)

        interleave_x(0)
        interleave_x(1)
        quantize_x(0)
        quantize_x(1)
        scores(0)
        scores(1)
        turn_plane(2)
        turn_plane(PACK - 1)
        load_y(2, 4 * SLOT)
        load_x(3, 5 * SLOT)
        load_y(3, 5 * SLOT + HALF)
        interleave_x(2)
        for s in range(CHUNKS + LAG + 1):
            each(scale_scores, s)
            each(residual, s)
            each(weigh, s - LAG)
            each(quantize_x, s + 2)
            each(scores, s + 2)
            if s + 1 >= EARLY and s + 1 not in STEPPED:
                each(deal_targets, s + 1)
            if s == 0:
                quantize_planes(1)
            done = s - LAG if s < CHUNKS - 1 else s - LAG - 1
            if s != CHUNKS - 1:
                each(quantize_h, done)
                each(gradient, done)
            each(squash, s)
            each(interleave_x, s + 3)
            if s != CHUNKS - 1:
                each(store, done)
